import numpy as np
import ml_dtypes


def mxq(x, axis, fmt="e4m3"):
    dtype, down = {"e4m3": (ml_dtypes.float8_e4m3fn, 7), "e5m2": (ml_dtypes.float8_e5m2, 14)}[fmt]
    v = np.moveaxis(np.asarray(x, np.float32).astype(ml_dtypes.bfloat16).astype(np.float64), axis, -1)
    blocks = v.reshape(v.shape[:-1] + (-1, 32))
    amax = np.abs(blocks).max(-1, keepdims=True)
    byte = np.maximum(np.where(amax > 0, np.frexp(amax)[1] - 1 + 127, 0) - down, 1)
    scale = np.exp2(byte - 127.0)
    codes = (blocks / scale).astype(np.float32).astype(dtype).astype(np.float64)
    return np.moveaxis((codes * scale).reshape(v.shape), -1, axis)


WIDE = False


def mx_kscale(k):
    if not WIDE:
        return np.ones(k)
    levels = np.array([10, -10, 5, -5, 0])
    if k % 512:
        return np.exp2(np.random.permutation(np.resize(levels, k // 32))).repeat(32)
    a = np.empty((k // 512, 16))
    for p in range(k // 512):
        a[p, :8] = np.random.permutation(np.resize(levels, 8))
        for g in range(8):
            far = levels[np.abs(levels - a[p, g]) >= 10]
            a[p, g + 8] = far[np.random.randint(len(far))]
    return np.exp2(a.ravel()).repeat(32)


def f64(x):
    return np.asarray(x).astype(np.float64)


def striped(idx):
    return np.tile(np.asarray(idx).reshape(-1, 16).T, (8, 1)).astype(np.uint16)


def unstriped(offs):
    return offs[:16].T.reshape(-1).astype(np.int64)


E2M1 = np.array([0.0, 0.5, 1.0, 1.5, 2.0, 3.0, 4.0, 6.0, -0.0, -0.5, -1.0, -1.5, -2.0, -3.0, -4.0, -6.0])


def pack_weight(w, fmt):
    k, n = w.shape
    w = f64(np.asarray(w, np.float32).astype(ml_dtypes.bfloat16)).reshape(k // 32, 32, n)
    amax = np.abs(w).max(1)
    if fmt == "e4m3":
        byte = np.frexp(amax)[1] - 1 + 127 - 7
    else:
        mant, ex = np.frexp(amax / 6.0)
        byte = np.where(mant > 0.5, ex, ex - 1) + 127
    byte = np.clip(np.where(amax > 0, byte, 1), 1, 254)
    scaled = (w * np.exp2(127.0 - byte)[:, None, :]).reshape(k, n).astype(np.float32)
    by_word = np.ascontiguousarray(scaled.reshape(k // 512, 128, 4, n).transpose(0, 1, 3, 2))
    if fmt == "e4m3":
        words = by_word.astype(ml_dtypes.float8_e4m3fn).view(np.uint8)
    else:
        c = by_word.astype(ml_dtypes.float4_e2m1fn).view(np.uint8) & 0xF
        words = (c[..., 0::2] | (c[..., 1::2] << 4)).reshape(k // 512, 128, 2 * n)
    return np.ascontiguousarray(words), np.ascontiguousarray(byte.astype(np.uint8).reshape(k // 512, 16, n))


def unpack_weight(words, scales, fmt):
    g, _, n = scales.shape
    words = np.ascontiguousarray(words).reshape(g, 128, n, -1)
    if fmt == "e4m3":
        vals = words.view(ml_dtypes.float8_e4m3fn).astype(np.float64)
    else:
        nib = np.empty((g, 128, n, 4), np.uint8)
        nib[..., 0::2] = words & 0xF
        nib[..., 1::2] = words >> 4
        vals = E2M1[nib]
    vals = vals * np.repeat(np.exp2(scales.astype(np.float64) - 127.0), 8, axis=1)[..., None]
    return vals.transpose(0, 1, 3, 2).reshape(g * 512, n)


B, N, T, D, DV, NQ = 1, 1536, 4096, 512, 256, 128
PAGE = 512


def setup_inputs():
    n = np.random.standard_normal
    pages = np.random.permutation(T // PAGE)[:B * N // PAGE]
    idx = (pages[:, None] * PAGE + np.arange(PAGE)[None, :]).reshape(-1)
    s = mx_kscale(D)[:, None]
    u = np.ones(T)
    u[idx] = mx_kscale(B * N)
    r = np.random.uniform(0.5, 2.0, T)
    qp = [pack_weight(x, "e4m3") for x in n((B, D, NQ)) * s * (0.60 / np.sqrt(D))]
    k = n((D, T)) / s
    v = n((DV, T)) / (u * r)
    kp = pack_weight(k, "e4m3")
    vp = pack_weight(v.T, "e4m3")
    return {
        "q_words": np.stack([x[0] for x in qp]),
        "q_scales": np.stack([x[1] for x in qp]),
        "k_words": kp[0],
        "k_scales": kp[1],
        "v_words": vp[0],
        "v_scales": vp[1],
        "vs": np.tile(u * r, (128, 1)).astype(np.float32),
        "offs": striped(idx),
        "voffs": striped((pages[:, None] * DV + np.arange(DV)[None, :]).reshape(-1)),
    }


def reference(q_words, q_scales, k_words, k_scales, v_words, v_scales, vs, offs, voffs):
    idx = unstriped(offs)
    k = unpack_weight(k_words, k_scales, "e4m3")
    v = unpack_weight(v_words, v_scales, "e4m3")
    v = v.reshape(T // 512, 512, DV)[unstriped(voffs)[::DV] // DV].reshape(B, N, DV)
    pick = lambda x: x[:, idx].reshape(x.shape[0], B, N).transpose(1, 0, 2)
    q = np.stack([unpack_weight(q_words[b], q_scales[b], "e4m3") for b in range(B)])
    score = q.transpose(0, 2, 1) @ pick(k)
    m = score.max(-1, keepdims=True)
    p = np.exp(score - m)
    total = p.sum(-1, keepdims=True)
    w = p * pick(f64(vs))[:, :1, :]
    y = mxq(w, 2, "e4m3") @ v
    y = y / total
    return y

@@ -1,0 +1,146 @@
+from contextlib import ExitStack
+
+import concourse.mybir as mybir
+from concourse.masks import make_identity
+
+F32 = mybir.dt.float32
+BF16 = mybir.dt.bfloat16
+I32 = mybir.dt.int32
+U32 = mybir.dt.uint32
+U16 = mybir.dt.uint16
+U8 = mybir.dt.uint8
+FP8X4 = mybir.dt.float8_e4m3fn_x4
+ALU = mybir.AluOpType
+ACT = mybir.ActivationFunctionType
+
+P = 128
+T = 4096
+NQ = 128
+DV = 256
+PAGE = 512
+PAGES = 3
+POOL_PAGES = 8
+PACK = 4
+FLOPS = 301989888
+
+
+def tile_attend_pkv8_qpk_kernel(tc, q_words, q_scales, k_words, k_scales, v_words, v_scales, vs, offs, voffs, out):
+    nc = tc.nc
+    with ExitStack() as ctx:
+        sb = ctx.enter_context(tc.tile_pool(name="sb", bufs=1))
+        ps = ctx.enter_context(tc.psum_pool(name="ps", bufs=1))
+
+        k_list = sb.tile([P, PAGES * PAGE // 16], U16, name="k_list")
+        v_list = sb.tile([P, PAGES * DV // 16], U16, name="v_list")
+        k_pool = sb.tile([P, T], I32, name="k_pool", align_bytes=64)
+        ks_pool = sb.tile([P, T], U8, name="ks_pool", align_bytes=64)
+        v_pool = sb.tile([P, POOL_PAGES * DV], I32, name="v_pool", align_bytes=64)
+        vb_pool = sb.tile([P, POOL_PAGES * DV], U8, name="vb_pool", align_bytes=64)
+        ts_pool = sb.tile([P, T], F32, name="ts_pool", align_bytes=64)
+        q_codes = sb.tile([P, NQ], I32, name="q_codes", align_bytes=64)
+        q_bytes = sb.tile([P, NQ], U8, name="q_bytes", align_bytes=64)
+        ident = sb.tile([P, P], F32, name="ident", align_bytes=64)
+        warm = sb.tile([P, 1], F32, name="warm")
+        warm2 = sb.tile([P, 1], F32, name="warm2")
+
+        nc.vector.memset(ks_pool[:].bitcast(I32), 0)
+        nc.vector.memset(vb_pool[:].bitcast(I32), 0)
+        nc.gpsimd.memset(q_bytes[:], 0)
+        nc.gpsimd.memset(warm[:], 0.0)
+        nc.scalar.activation(out=warm2[:], in_=warm[:], func=ACT.Exp)
+
+        nc.sync.dma_start(k_list[:], offs)
+        for Q in range(4):
+            nc.scalar.dma_start(out=ks_pool[32 * Q : 32 * Q + 4, :].bitcast(I32), in_=k_scales[0, 4 * Q : 4 * Q + 4, :].bitcast(I32))
+        nc.sync.dma_start(out=k_pool[:], in_=k_words[0].rearrange("p t r -> p (t r)").bitcast(I32))
+        nc.sync.dma_start(out=q_codes[:], in_=q_words[0, 0].rearrange("p q r -> p (q r)").bitcast(I32))
+        nc.sync.dma_start(v_list[:], voffs)
+        for Q in range(4):
+            nc.gpsimd.dma_start(out=q_bytes[32 * Q : 32 * Q + 4, :].bitcast(I32), in_=q_scales[0, 0, 4 * Q : 4 * Q + 4, :].bitcast(I32))
+        make_identity(nc, ident[:])
+        for Q in range(4):
+            nc.sync.dma_start(
+                out=vb_pool[32 * Q : 32 * Q + 4, :].bitcast(I32).rearrange("p (u e) -> p u e", u=POOL_PAGES),
+                in_=v_scales[:, 4 * Q : 4 * Q + 4, :].rearrange("u f e -> f u e").bitcast(I32),
+            )
+        nc.sync.dma_start(out=ts_pool[:], in_=vs)
+        nc.sync.dma_start(
+            out=v_pool[:].rearrange("p (u e) -> p u e", u=POOL_PAGES),
+            in_=v_words.rearrange("u p e r -> p u (e r)").bitcast(I32),
+        )
+
+        k_bytes = sb.tile([P, PAGES * PAGE], U8, name="k_bytes", align_bytes=64)
+        nc.vector.tensor_copy(k_bytes[:], ks_pool[:].indirect(k_list[:]))
+
+        kc = PAGE // 16
+        vc = DV // 16
+        scores = []
+        neg_max = []
+        junk = sb.tile([P, PAGE], F32, name="junk")
+
+        def row_max(g):
+            nm = sb.tile([P, 1], F32, name=f"neg_max{g}")
+            nc.vector.tensor_scalar(
+                out=junk[:], in0=scores[g][:], scalar1=-1.0, scalar2=(neg_max[g - 1][:] if g else None),
+                op0=ALU.mult, op1=ALU.min, accum_out=nm[:],
+            )
+            neg_max.append(nm)
+
+        v_bytes = []
+
+        def gather_vb(g):
+            vb = sb.tile([P, DV], U8, name=f"v_bytes{g}", align_bytes=64)
+            nc.vector.tensor_copy(vb[:], vb_pool[:].indirect(v_list[:, g * vc : (g + 1) * vc]))
+            v_bytes.append(vb)
+
+        for g in range(PAGES):
+            k_codes = sb.tile([P, PAGE], U32, name=f"k_codes{g}", align_bytes=64)
+            nc.vector.tensor_copy(k_codes[:], k_pool[:].bitcast(U32).indirect(k_list[:, g * kc : (g + 1) * kc]))
+            bank = ps.tile([P, PAGE], F32, name=f"score{g}")
+            nc.tensor.matmul_mx(
+                out=bank[:], lhsT=q_codes[:].bitcast(FP8X4), lhsT_scale=q_bytes[:],
+                rhs=k_codes[:].bitcast(FP8X4), rhs_scale=k_bytes[:, g * PAGE : (g + 1) * PAGE],
+                start=True, stop=True,
+            )
+            scores.append(bank)
+            if g > 0:
+                row_max(g - 1)
+        gather_vb(0)
+        row_max(PAGES - 1)
+        gather_vb(1)
+
+        sums = sb.tile([P, PAGES], F32, name="sums")
+        w_bf = []
+        for g in range(PAGES):
+            p = sb.tile([P, PAGE], F32, name=f"p{g}", align_bytes=64)
+            nc.scalar.activation(out=p[:], in_=scores[g][:], func=ACT.Exp, bias=neg_max[PAGES - 1][:], scale=1.0, accum_out=sums[:, g : g + 1])
+            w = sb.tile([P, PAGE], F32, name=f"w{g}", align_bytes=64)
+            nc.vector.tensor_tensor(w[:], ts_pool[:].indirect(k_list[:, g * kc : (g + 1) * kc]), p[:], ALU.mult)
+            turned = ps.tile([P, PACK, NQ], F32, name=f"turned{g}")
+            for t in range(PACK):
+                nc.tensor.transpose(turned[:, t, :], w[:, t:PAGE:PACK], ident[:])
+            wb = sb.tile([P, NQ, PACK], BF16, name=f"w_bf{g}", align_bytes=64)
+            nc.scalar.copy(out=wb[:], in_=turned[:].rearrange("p t q -> p q t"))
+            w_bf.append(wb)
+
+        total = sb.tile([P, 1], F32, name="total")
+        inv = sb.tile([P, 1], F32, name="inv")
+        nc.vector.tensor_reduce(out=total[:], in_=sums[:], axis=mybir.AxisListType.X, op=ALU.add)
+        v_codes = sb.tile([P, PAGES * DV], U32, name="v_codes", align_bytes=64)
+        nc.vector.tensor_copy(v_codes[:], v_pool[:].bitcast(U32).indirect(v_list[:]))
+        nc.vector.reciprocal(inv[:], total[:])
+        gather_vb(2)
+
+        acc = ps.tile([P, DV], F32, name="acc")
+        for g in range(PAGES):
+            w_codes = sb.tile([P, NQ], U32, name=f"w_codes{g}", align_bytes=64)
+            w_bytes = sb.tile([P, NQ], U8, name=f"w_bytes{g}", align_bytes=64)
+            nc.vector.quantize_mx(out=w_codes[:].bitcast(FP8X4), scales=w_bytes[:], in_=w_bf[g][:].rearrange("p q t -> p (q t)"))
+            nc.tensor.matmul_mx(
+                out=acc[:], lhsT=w_codes[:].bitcast(FP8X4), lhsT_scale=w_bytes[:],
+                rhs=v_codes[:, g * DV : (g + 1) * DV].bitcast(FP8X4), rhs_scale=v_bytes[g][:],
+                start=(g == 0), stop=(g == PAGES - 1),
+            )
+        y = sb.tile([P, DV], F32, name="y")
+        nc.scalar.activation(out=y[:], in_=acc[:], func=ACT.Copy, scale=inv[:])
+        nc.sync.dma_start(out=out[0], in_=y[:])

@@ -1,7 +1,6 @@
 from contextlib import ExitStack
 
 import concourse.mybir as mybir
-from concourse.masks import make_identity
 
 F32 = mybir.dt.float32
 BF16 = mybir.dt.bfloat16
@@ -28,71 +27,73 @@ def tile_attend_pkv8_qpk_kernel(tc, q_words, q_scales, k_words, k_scales, v_word
     nc = tc.nc
     with ExitStack() as ctx:
         sb = ctx.enter_context(tc.tile_pool(name="sb", bufs=1))
+        laid = ctx.enter_context(tc.tile_pool(name="laid", bufs=1))
         ps = ctx.enter_context(tc.psum_pool(name="ps", bufs=1))
 
         k_list = sb.tile([P, PAGES * PAGE // 16], U16, name="k_list")
         v_list = sb.tile([P, PAGES * DV // 16], U16, name="v_list")
-        k_pool = sb.tile([P, T], I32, name="k_pool", align_bytes=64)
-        ks_pool = sb.tile([P, T], U8, name="ks_pool", align_bytes=64)
-        v_pool = sb.tile([P, POOL_PAGES * DV], I32, name="v_pool", align_bytes=64)
-        vb_pool = sb.tile([P, POOL_PAGES * DV], U8, name="vb_pool", align_bytes=64)
         ts_pool = sb.tile([P, T], F32, name="ts_pool", align_bytes=64)
-        q_codes = sb.tile([P, NQ], I32, name="q_codes", align_bytes=64)
-        q_bytes = sb.tile([P, NQ], U8, name="q_bytes", align_bytes=64)
+        ts_cols = sb.tile([P, T // P], F32, name="ts_cols", align_bytes=64)
         ident = sb.tile([P, P], F32, name="ident", align_bytes=64)
-        warm = sb.tile([P, 1], F32, name="warm")
         warm2 = sb.tile([P, 1], F32, name="warm2")
 
-        nc.vector.memset(ks_pool[:].bitcast(I32), 0)
-        nc.vector.memset(vb_pool[:].bitcast(I32), 0)
-        nc.gpsimd.memset(q_bytes[:], 0)
+        at_qb = 4 * T
+        at_qc = at_qb + NQ
+        at_vb = at_qc + 4 * NQ
+        at_ks = at_vb + POOL_PAGES * DV
+        ks_pool = laid.tile([P, T], U8, name="ks_pool", align_bytes=64, offset=at_ks)
+        ones = laid.tile([P, P], F32, name="ones", align_bytes=64, offset=at_qb - 64)
+        warm = laid.tile([P, 1], F32, name="warm", align_bytes=64, offset=at_vb)
+
         nc.gpsimd.memset(warm[:], 0.0)
         nc.scalar.activation(out=warm2[:], in_=warm[:], func=ACT.Exp)
+        nc.gpsimd.memset(ks_pool[:, : T // 2].bitcast(I32), 0)
+        nc.vector.memset(ks_pool[:, T // 2 :].bitcast(I32), 0)
+        nc.vector.memset(ones[:], 1.0)
+        nc.gpsimd.affine_select(out=ident[:], in_=ones[:], pattern=[[-1, P]], compare_op=ALU.is_equal, fill=0.0, base=0, channel_multiplier=1)
 
         nc.sync.dma_start(k_list[:], offs)
-        for Q in range(4):
-            nc.scalar.dma_start(out=ks_pool[32 * Q : 32 * Q + 4, :].bitcast(I32), in_=k_scales[0, 4 * Q : 4 * Q + 4, :].bitcast(I32))
-        nc.sync.dma_start(out=k_pool[:], in_=k_words[0].rearrange("p t r -> p (t r)").bitcast(I32))
-        nc.sync.dma_start(out=q_codes[:], in_=q_words[0, 0].rearrange("p q r -> p (q r)").bitcast(I32))
+        nc.sync.dma_start(out=ts_cols[:], in_=vs[0].rearrange("(p c) -> p c", p=P))
         nc.sync.dma_start(v_list[:], voffs)
         for Q in range(4):
-            nc.gpsimd.dma_start(out=q_bytes[32 * Q : 32 * Q + 4, :].bitcast(I32), in_=q_scales[0, 0, 4 * Q : 4 * Q + 4, :].bitcast(I32))
-        make_identity(nc, ident[:])
+            nc.sync.dma_start(out=ks_pool[32 * Q : 32 * Q + 4, :].bitcast(I32), in_=k_scales[0, 4 * Q : 4 * Q + 4, :].bitcast(I32))
+        k_pool = laid.tile([P, T], I32, name="k_pool", align_bytes=64, offset=0)
+        nc.sync.dma_start(out=k_pool[:], in_=k_words[0].rearrange("p t r -> p (t r)").bitcast(I32))
+        q_codes = laid.tile([P, NQ], I32, name="q_codes", align_bytes=64, offset=at_qc)
+        nc.sync.dma_start(out=q_codes[:], in_=q_words[0, 0].rearrange("p q r -> p (q r)").bitcast(I32))
+        q_bytes = laid.tile([P, NQ], U8, name="q_bytes", align_bytes=64, offset=at_qb)
+        nc.gpsimd.memset(q_bytes[:].bitcast(I32), 0)
+        for Q in range(4):
+            nc.sync.dma_start(out=q_bytes[32 * Q : 32 * Q + 4, :].bitcast(I32), in_=q_scales[0, 0, 4 * Q : 4 * Q + 4, :].bitcast(I32))
+        vb_pool = laid.tile([P, POOL_PAGES * DV], U8, name="vb_pool", align_bytes=64, offset=at_vb)
+        nc.gpsimd.memset(vb_pool[:].bitcast(I32), 0)
         for Q in range(4):
             nc.sync.dma_start(
                 out=vb_pool[32 * Q : 32 * Q + 4, :].bitcast(I32).rearrange("p (u e) -> p u e", u=POOL_PAGES),
                 in_=v_scales[:, 4 * Q : 4 * Q + 4, :].rearrange("u f e -> f u e").bitcast(I32),
             )
-        nc.sync.dma_start(out=ts_pool[:], in_=vs)
+
+        per = T // P
+        ts_view = ts_pool[:].rearrange("p (i b c) -> p b i c", b=per // PACK, c=PACK)
+        for b in range(per // PACK):
+            spread = ps.tile([P, PACK, P], F32, name=f"spread{b}", tag=f"turn{b % 4}")
+            for c in range(PACK):
+                col = PACK * b + c
+                nc.tensor.transpose(spread[:, c, :], ts_cols[:, col : col + 1].to_broadcast([P, P]), ident[:])
+            nc.scalar.activation(out=ts_view[:, b], in_=spread[:].rearrange("p c i -> p i c"), func=ACT.Copy)
+
+        k_bytes = sb.tile([P, PAGES * PAGE], U8, name="k_bytes", align_bytes=64)
+        nc.vector.tensor_copy(k_bytes[:], ks_pool[:].indirect(k_list[:]))
+
+        v_pool = laid.tile([P, POOL_PAGES * DV], I32, name="v_pool", align_bytes=64, offset=at_ks)
         nc.sync.dma_start(
             out=v_pool[:].rearrange("p (u e) -> p u e", u=POOL_PAGES),
             in_=v_words.rearrange("u p e r -> p u (e r)").bitcast(I32),
         )
 
-        k_bytes = sb.tile([P, PAGES * PAGE], U8, name="k_bytes", align_bytes=64)
-        nc.vector.tensor_copy(k_bytes[:], ks_pool[:].indirect(k_list[:]))
-
         kc = PAGE // 16
         vc = DV // 16
         scores = []
-        neg_max = []
-        junk = sb.tile([P, PAGE], F32, name="junk")
-
-        def row_max(g):
-            nm = sb.tile([P, 1], F32, name=f"neg_max{g}")
-            nc.vector.tensor_scalar(
-                out=junk[:], in0=scores[g][:], scalar1=-1.0, scalar2=(neg_max[g - 1][:] if g else None),
-                op0=ALU.mult, op1=ALU.min, accum_out=nm[:],
-            )
-            neg_max.append(nm)
-
-        v_bytes = []
-
-        def gather_vb(g):
-            vb = sb.tile([P, DV], U8, name=f"v_bytes{g}", align_bytes=64)
-            nc.vector.tensor_copy(vb[:], vb_pool[:].indirect(v_list[:, g * vc : (g + 1) * vc]))
-            v_bytes.append(vb)
-
         for g in range(PAGES):
             k_codes = sb.tile([P, PAGE], U32, name=f"k_codes{g}", align_bytes=64)
             nc.vector.tensor_copy(k_codes[:], k_pool[:].bitcast(U32).indirect(k_list[:, g * kc : (g + 1) * kc]))
@@ -103,44 +104,66 @@ def tile_attend_pkv8_qpk_kernel(tc, q_words, q_scales, k_words, k_scales, v_word
                 start=True, stop=True,
             )
             scores.append(bank)
-            if g > 0:
-                row_max(g - 1)
-        gather_vb(0)
-        row_max(PAGES - 1)
-        gather_vb(1)
+
+        negated = sb.tile([P, PAGE], F32, name="negated", tag="negated", align_bytes=64)
+        neg_max = None
+        for g in range(PAGES):
+            running = sb.tile([P, 1], F32, name=f"neg_max{g}")
+            nc.vector.tensor_scalar(
+                out=negated[:], in0=scores[g][:], scalar1=-1.0, scalar2=neg_max,
+                op0=ALU.mult, op1=ALU.min, accum_out=running[:],
+            )
+            neg_max = running[:]
+
+        vb_first = sb.tile([P, DV], U8, name="vb_first", tag="negated", align_bytes=64)
+        nc.vector.tensor_copy(vb_first[:], vb_pool[:].indirect(v_list[:, :vc]))
 
         sums = sb.tile([P, PAGES], F32, name="sums")
         w_bf = []
         for g in range(PAGES):
-            p = sb.tile([P, PAGE], F32, name=f"p{g}", align_bytes=64)
-            nc.scalar.activation(out=p[:], in_=scores[g][:], func=ACT.Exp, bias=neg_max[PAGES - 1][:], scale=1.0, accum_out=sums[:, g : g + 1])
+            p = sb.tile([P, PAGE], F32, name=f"p{g}", tag=f"p{g}", align_bytes=64)
+            nc.scalar.activation(out=p[:], in_=scores[g][:], func=ACT.Exp, bias=neg_max, scale=1.0, accum_out=sums[:, g : g + 1])
             w = sb.tile([P, PAGE], F32, name=f"w{g}", align_bytes=64)
             nc.vector.tensor_tensor(w[:], ts_pool[:].indirect(k_list[:, g * kc : (g + 1) * kc]), p[:], ALU.mult)
-            turned = ps.tile([P, PACK, NQ], F32, name=f"turned{g}")
+            turned = ps.tile([P, PACK, NQ], F32, name=f"turned{g}", tag=f"turn{g}")
             for t in range(PACK):
                 nc.tensor.transpose(turned[:, t, :], w[:, t:PAGE:PACK], ident[:])
-            wb = sb.tile([P, NQ, PACK], BF16, name=f"w_bf{g}", align_bytes=64)
+            wb = sb.tile([P, NQ, PACK], BF16, name=f"w_bf{g}", tag=f"w_bf{g}", align_bytes=64)
             nc.scalar.copy(out=wb[:], in_=turned[:].rearrange("p t q -> p q t"))
             w_bf.append(wb)
 
+        v_early = sb.tile([P, 2 * DV], U32, name="v_early", tag="p2", align_bytes=64)
+        nc.vector.tensor_copy(v_early[:], v_pool[:].bitcast(U32).indirect(v_list[:, : 2 * vc]))
+
+        w_codes = [sb.tile([P, NQ], U32, name=f"w_codes{g}", align_bytes=64) for g in range(PAGES)]
+        w_bytes = [sb.tile([P, NQ], U8, name=f"w_bytes{g}", align_bytes=64) for g in range(PAGES)]
+
+        def quantise(g):
+            nc.vector.quantize_mx(out=w_codes[g][:].bitcast(FP8X4), scales=w_bytes[g][:], in_=w_bf[g][:].rearrange("p q t -> p (q t)"))
+
+        acc = ps.tile([P, DV], F32, name="acc")
+
+        def product(g, codes, scale_bytes):
+            nc.tensor.matmul_mx(
+                out=acc[:], lhsT=w_codes[g][:].bitcast(FP8X4), lhsT_scale=w_bytes[g][:],
+                rhs=codes.bitcast(FP8X4), rhs_scale=scale_bytes,
+                start=(g == 0), stop=(g == PAGES - 1),
+            )
+
+        quantise(0)
+        product(0, v_early[:, :DV], vb_first[:])
+        vb_rest = sb.tile([P, 2 * DV], U8, name="vb_rest", tag="p1", align_bytes=64)
+        nc.vector.tensor_copy(vb_rest[:], vb_pool[:].indirect(v_list[:, vc:]))
+        quantise(1)
+        product(1, v_early[:, DV:], vb_rest[:, :DV])
         total = sb.tile([P, 1], F32, name="total")
         inv = sb.tile([P, 1], F32, name="inv")
         nc.vector.tensor_reduce(out=total[:], in_=sums[:], axis=mybir.AxisListType.X, op=ALU.add)
-        v_codes = sb.tile([P, PAGES * DV], U32, name="v_codes", align_bytes=64)
-        nc.vector.tensor_copy(v_codes[:], v_pool[:].bitcast(U32).indirect(v_list[:]))
+        quantise(2)
         nc.vector.reciprocal(inv[:], total[:])
-        gather_vb(2)
-
-        acc = ps.tile([P, DV], F32, name="acc")
-        for g in range(PAGES):
-            w_codes = sb.tile([P, NQ], U32, name=f"w_codes{g}", align_bytes=64)
-            w_bytes = sb.tile([P, NQ], U8, name=f"w_bytes{g}", align_bytes=64)
-            nc.vector.quantize_mx(out=w_codes[:].bitcast(FP8X4), scales=w_bytes[:], in_=w_bf[g][:].rearrange("p q t -> p (q t)"))
-            nc.tensor.matmul_mx(
-                out=acc[:], lhsT=w_codes[:].bitcast(FP8X4), lhsT_scale=w_bytes[:],
-                rhs=v_codes[:, g * DV : (g + 1) * DV].bitcast(FP8X4), rhs_scale=v_bytes[g][:],
-                start=(g == 0), stop=(g == PAGES - 1),
-            )
+        v_last = sb.tile([P, DV], U32, name="v_last", tag="w_bf1", align_bytes=64)
+        nc.vector.tensor_copy(v_last[:], v_pool[:].bitcast(U32).indirect(v_list[:, 2 * vc :]))
+        product(2, v_last[:], vb_rest[:, DV:])
         y = sb.tile([P, DV], F32, name="y")
         nc.scalar.activation(out=y[:], in_=acc[:], func=ACT.Copy, scale=inv[:])
         nc.sync.dma_start(out=out[0], in_=y[:])

@@ -45,20 +45,25 @@ def tile_attend_pkv8_qpk_kernel(tc, q_words, q_scales, k_words, k_scales, v_word
         ones = laid.tile([P, P], F32, name="ones", align_bytes=64, offset=at_qb - 64)
         warm = laid.tile([P, 1], F32, name="warm", align_bytes=64, offset=at_vb)
 
-        nc.gpsimd.memset(warm[:], 0.0)
-        nc.scalar.activation(out=warm2[:], in_=warm[:], func=ACT.Exp)
         nc.gpsimd.memset(ks_pool[:, : T // 2].bitcast(I32), 0)
         nc.vector.memset(ks_pool[:, T // 2 :].bitcast(I32), 0)
         nc.vector.memset(ones[:], 1.0)
+        nc.vector.memset(warm[:], 0.0)
+        nc.scalar.activation(out=warm2[:], in_=warm[:], func=ACT.Exp)
         nc.gpsimd.affine_select(out=ident[:], in_=ones[:], pattern=[[-1, P]], compare_op=ALU.is_equal, fill=0.0, base=0, channel_multiplier=1)
 
+        k_rows = k_words[0].rearrange("p t r -> p (t r)").bitcast(I32)
+        head = T // 4
+        k_head = sb.tile([P, head], I32, name="k_head", align_bytes=64)
         nc.sync.dma_start(k_list[:], offs)
         nc.sync.dma_start(out=ts_cols[:], in_=vs[0].rearrange("(p c) -> p c", p=P))
+        nc.sync.dma_start(out=k_head[:], in_=k_rows[:, :head])
         nc.sync.dma_start(v_list[:], voffs)
         for Q in range(4):
             nc.sync.dma_start(out=ks_pool[32 * Q : 32 * Q + 4, :].bitcast(I32), in_=k_scales[0, 4 * Q : 4 * Q + 4, :].bitcast(I32))
         k_pool = laid.tile([P, T], I32, name="k_pool", align_bytes=64, offset=0)
-        nc.sync.dma_start(out=k_pool[:], in_=k_words[0].rearrange("p t r -> p (t r)").bitcast(I32))
+        nc.sync.dma_start(out=k_pool[:, head:], in_=k_rows[:, head:])
+        nc.vector.tensor_copy(k_pool[:, :head], k_head[:])
         q_codes = laid.tile([P, NQ], I32, name="q_codes", align_bytes=64, offset=at_qc)
         nc.sync.dma_start(out=q_codes[:], in_=q_words[0, 0].rearrange("p q r -> p (q r)").bitcast(I32))
         q_bytes = laid.tile([P, NQ], U8, name="q_bytes", align_bytes=64, offset=at_qb)
@@ -105,31 +110,30 @@ def tile_attend_pkv8_qpk_kernel(tc, q_words, q_scales, k_words, k_scales, v_word
             )
             scores.append(bank)
 
-        negated = sb.tile([P, PAGE], F32, name="negated", tag="negated", align_bytes=64)
-        neg_max = None
+        page_max = sb.tile([P, PAGES], F32, name="page_max", tag="page_max", align_bytes=64)
         for g in range(PAGES):
-            running = sb.tile([P, 1], F32, name=f"neg_max{g}")
-            nc.vector.tensor_scalar(
-                out=negated[:], in0=scores[g][:], scalar1=-1.0, scalar2=neg_max,
-                op0=ALU.mult, op1=ALU.min, accum_out=running[:],
-            )
-            neg_max = running[:]
+            nc.vector.tensor_reduce(out=page_max[:, g : g + 1], in_=scores[g][:], axis=mybir.AxisListType.X, op=ALU.max)
+        neg_max = sb.tile([P, 1], F32, name="neg_max")
+        nc.vector.tensor_reduce(out=neg_max[:], in_=page_max[:], axis=mybir.AxisListType.X, op=ALU.max, negate=True)
 
-        vb_first = sb.tile([P, DV], U8, name="vb_first", tag="negated", align_bytes=64)
-        nc.vector.tensor_copy(vb_first[:], vb_pool[:].indirect(v_list[:, :vc]))
+        vb_early = sb.tile([P, 2 * DV], U8, name="vb_early", tag="page_max", align_bytes=64)
+        nc.vector.tensor_copy(vb_early[:], vb_pool[:].indirect(v_list[:, : 2 * vc]))
 
         sums = sb.tile([P, PAGES], F32, name="sums")
         w_bf = []
         for g in range(PAGES):
             p = sb.tile([P, PAGE], F32, name=f"p{g}", tag=f"p{g}", align_bytes=64)
-            nc.scalar.activation(out=p[:], in_=scores[g][:], func=ACT.Exp, bias=neg_max, scale=1.0, accum_out=sums[:, g : g + 1])
+            nc.scalar.activation(out=p[:], in_=scores[g][:], func=ACT.Exp, bias=neg_max[:], scale=1.0, accum_out=sums[:, g : g + 1])
             w = sb.tile([P, PAGE], F32, name=f"w{g}", align_bytes=64)
             nc.vector.tensor_tensor(w[:], ts_pool[:].indirect(k_list[:, g * kc : (g + 1) * kc]), p[:], ALU.mult)
-            turned = ps.tile([P, PACK, NQ], F32, name=f"turned{g}", tag=f"turn{g}")
-            for t in range(PACK):
-                nc.tensor.transpose(turned[:, t, :], w[:, t:PAGE:PACK], ident[:])
-            wb = sb.tile([P, NQ, PACK], BF16, name=f"w_bf{g}", tag=f"w_bf{g}", align_bytes=64)
-            nc.scalar.copy(out=wb[:], in_=turned[:].rearrange("p t q -> p q t"))
+            pairs = sb.tile([P, 2, P, 2], BF16, name=f"pairs{g}", align_bytes=64)
+            nc.scalar.copy(out=pairs[:], in_=w[:].rearrange("q (s u e) -> q u s e", u=2, e=2))
+            pair_words = pairs[:].rearrange("q u s e -> q (u s e)").bitcast(F32)
+            turned = ps.tile([P, 2, NQ], F32, name=f"turned{g}", tag=f"turn{g}")
+            for u in range(2):
+                nc.tensor.transpose(turned[:, u, :], pair_words[:, u * P : (u + 1) * P], ident[:])
+            wb = sb.tile([P, NQ * PACK], BF16, name=f"w_bf{g}", tag=f"w_bf{g}", align_bytes=64)
+            nc.scalar.copy(out=wb[:].bitcast(F32).rearrange("s (q u) -> s q u", u=2), in_=turned[:].rearrange("s u q -> s q u"))
             w_bf.append(wb)
 
         v_early = sb.tile([P, 2 * DV], U32, name="v_early", tag="p2", align_bytes=64)
@@ -139,31 +143,37 @@ def tile_attend_pkv8_qpk_kernel(tc, q_words, q_scales, k_words, k_scales, v_word
         w_bytes = [sb.tile([P, NQ], U8, name=f"w_bytes{g}", align_bytes=64) for g in range(PAGES)]
 
         def quantise(g):
-            nc.vector.quantize_mx(out=w_codes[g][:].bitcast(FP8X4), scales=w_bytes[g][:], in_=w_bf[g][:].rearrange("p q t -> p (q t)"))
+            nc.vector.quantize_mx(out=w_codes[g][:].bitcast(FP8X4), scales=w_bytes[g][:], in_=w_bf[g][:])
 
-        acc = ps.tile([P, DV], F32, name="acc")
+        half = DV // 2
+        acc = [ps.tile([P, half], F32, name=f"acc{h}", tag=("acc", "turn3")[h]) for h in range(2)]
 
         def product(g, codes, scale_bytes):
-            nc.tensor.matmul_mx(
-                out=acc[:], lhsT=w_codes[g][:].bitcast(FP8X4), lhsT_scale=w_bytes[g][:],
-                rhs=codes.bitcast(FP8X4), rhs_scale=scale_bytes,
-                start=(g == 0), stop=(g == PAGES - 1),
-            )
+            for h in range(2):
+                nc.tensor.matmul_mx(
+                    out=acc[h][:], lhsT=w_codes[g][:].bitcast(FP8X4), lhsT_scale=w_bytes[g][:],
+                    rhs=codes[:, h * half : (h + 1) * half].bitcast(FP8X4), rhs_scale=scale_bytes[:, h * half : (h + 1) * half],
+                    start=(g == 0), stop=(g == PAGES - 1),
+                )
 
         quantise(0)
-        product(0, v_early[:, :DV], vb_first[:])
-        vb_rest = sb.tile([P, 2 * DV], U8, name="vb_rest", tag="p1", align_bytes=64)
-        nc.vector.tensor_copy(vb_rest[:], vb_pool[:].indirect(v_list[:, vc:]))
+        product(0, v_early[:, :DV], vb_early[:, :DV])
         quantise(1)
-        product(1, v_early[:, DV:], vb_rest[:, :DV])
+        product(1, v_early[:, DV:], vb_early[:, DV:])
         total = sb.tile([P, 1], F32, name="total")
         inv = sb.tile([P, 1], F32, name="inv")
-        nc.vector.tensor_reduce(out=total[:], in_=sums[:], axis=mybir.AxisListType.X, op=ALU.add)
-        quantise(2)
+        sums_again = sb.tile([P, PAGES], F32, name="sums_again")
+        nc.scalar.activation(out=sums_again[:], in_=sums[:], func=ACT.Identity, accum_out=total[:])
         nc.vector.reciprocal(inv[:], total[:])
+        vb_last = sb.tile([P, DV], U8, name="vb_last", tag="w_bf0", align_bytes=64)
+        nc.vector.tensor_copy(vb_last[:], vb_pool[:].indirect(v_list[:, 2 * vc :]))
         v_last = sb.tile([P, DV], U32, name="v_last", tag="w_bf1", align_bytes=64)
         nc.vector.tensor_copy(v_last[:], v_pool[:].bitcast(U32).indirect(v_list[:, 2 * vc :]))
-        product(2, v_last[:], vb_rest[:, DV:])
-        y = sb.tile([P, DV], F32, name="y")
-        nc.scalar.activation(out=y[:], in_=acc[:], func=ACT.Copy, scale=inv[:])
-        nc.sync.dma_start(out=out[0], in_=y[:])
+        quantise(2)
+        product(2, v_last[:], vb_last[:])
+        y0 = sb.tile([P, half], F32, name="y0")
+        y1 = sb.tile([P, half], F32, name="y1")
+        nc.scalar.activation(out=y0[:], in_=acc[0][:], func=ACT.Copy, scale=inv[:])
+        nc.vector.tensor_scalar(out=y1[:], in0=acc[1][:], scalar1=inv[:], scalar2=None, op0=ALU.mult)
+        nc.scalar.dma_start(out=out[0, :, :half], in_=y0[:])
+        nc.sync.dma_start(out=out[0, :, half:], in_=y1[:])

@@ -20,6 +20,7 @@ PAGE = 512
 PAGES = 3
 POOL_PAGES = 8
 PACK = 4
+VROW = 4
 FLOPS = 301989888
 
 
@@ -53,30 +54,26 @@ def tile_attend_pkv8_qpk_kernel(tc, q_words, q_scales, k_words, k_scales, v_word
         nc.gpsimd.affine_select(out=ident[:], in_=ones[:], pattern=[[-1, P]], compare_op=ALU.is_equal, fill=0.0, base=0, channel_multiplier=1)
 
         k_rows = k_words[0].rearrange("p t r -> p (t r)").bitcast(I32)
-        head = T // 4
-        k_head = sb.tile([P, head], I32, name="k_head", align_bytes=64)
         nc.sync.dma_start(k_list[:], offs)
-        nc.sync.dma_start(out=ts_cols[:], in_=vs[0].rearrange("(p c) -> p c", p=P))
-        nc.sync.dma_start(out=k_head[:], in_=k_rows[:, :head])
         nc.sync.dma_start(v_list[:], voffs)
-        for Q in range(4):
-            nc.sync.dma_start(out=ks_pool[32 * Q : 32 * Q + 4, :].bitcast(I32), in_=k_scales[0, 4 * Q : 4 * Q + 4, :].bitcast(I32))
+        nc.sync.dma_start(out=ts_cols[:], in_=vs[0].rearrange("(p c) -> p c", p=P))
+        for r in range(4):
+            nc.sync.dma_start(out=ks_pool[r:P:32, :].bitcast(I32), in_=k_scales[0, r:16:4, :].bitcast(I32))
         k_pool = laid.tile([P, T], I32, name="k_pool", align_bytes=64, offset=0)
-        nc.sync.dma_start(out=k_pool[:, head:], in_=k_rows[:, head:])
-        nc.vector.tensor_copy(k_pool[:, :head], k_head[:])
+        nc.sync.dma_start(out=k_pool[:], in_=k_rows)
+        vb_pool = sb.tile([P, POOL_PAGES * DV], U8, name="vb_pool", align_bytes=64)
+        nc.vector.memset(vb_pool[:].bitcast(I32), 0)
+        for r in range(4):
+            nc.scalar.dma_start(
+                out=vb_pool[VROW + r : P : 32, :].bitcast(I32).rearrange("p (u e) -> p u e", u=POOL_PAGES),
+                in_=v_scales[:, r:16:4, :].rearrange("u f e -> f u e").bitcast(I32),
+            )
         q_codes = laid.tile([P, NQ], I32, name="q_codes", align_bytes=64, offset=at_qc)
         nc.sync.dma_start(out=q_codes[:], in_=q_words[0, 0].rearrange("p q r -> p (q r)").bitcast(I32))
         q_bytes = laid.tile([P, NQ], U8, name="q_bytes", align_bytes=64, offset=at_qb)
         nc.gpsimd.memset(q_bytes[:].bitcast(I32), 0)
-        for Q in range(4):
-            nc.sync.dma_start(out=q_bytes[32 * Q : 32 * Q + 4, :].bitcast(I32), in_=q_scales[0, 0, 4 * Q : 4 * Q + 4, :].bitcast(I32))
-        vb_pool = laid.tile([P, POOL_PAGES * DV], U8, name="vb_pool", align_bytes=64, offset=at_vb)
-        nc.gpsimd.memset(vb_pool[:].bitcast(I32), 0)
-        for Q in range(4):
-            nc.sync.dma_start(
-                out=vb_pool[32 * Q : 32 * Q + 4, :].bitcast(I32).rearrange("p (u e) -> p u e", u=POOL_PAGES),
-                in_=v_scales[:, 4 * Q : 4 * Q + 4, :].rearrange("u f e -> f u e").bitcast(I32),
-            )
+        for r in range(4):
+            nc.gpsimd.dma_start(out=q_bytes[r:P:32, :].bitcast(I32), in_=q_scales[0, 0, r:16:4, :].bitcast(I32))
 
         per = T // P
         ts_view = ts_pool[:].rearrange("p (i b c) -> p b i c", b=per // PACK, c=PACK)
@@ -90,6 +87,9 @@ def tile_attend_pkv8_qpk_kernel(tc, q_words, q_scales, k_words, k_scales, v_word
         k_bytes = sb.tile([P, PAGES * PAGE], U8, name="k_bytes", align_bytes=64)
         nc.vector.tensor_copy(k_bytes[:], ks_pool[:].indirect(k_list[:]))
 
+        v_bytes = sb.tile([P, PAGES * DV], U8, name="v_bytes", align_bytes=64)
+        nc.vector.tensor_copy(v_bytes[:], vb_pool[:].indirect(v_list[:]))
+
         v_pool = laid.tile([P, POOL_PAGES * DV], I32, name="v_pool", align_bytes=64, offset=at_ks)
         nc.sync.dma_start(
             out=v_pool[:].rearrange("p (u e) -> p u e", u=POOL_PAGES),
@@ -97,7 +97,6 @@ def tile_attend_pkv8_qpk_kernel(tc, q_words, q_scales, k_words, k_scales, v_word
         )
 
         kc = PAGE // 16
-        vc = DV // 16
         scores = []
         for g in range(PAGES):
             k_codes = sb.tile([P, PAGE], U32, name=f"k_codes{g}", align_bytes=64)
@@ -110,67 +109,55 @@ def tile_attend_pkv8_qpk_kernel(tc, q_words, q_scales, k_words, k_scales, v_word
             )
             scores.append(bank)
 
-        page_max = sb.tile([P, PAGES], F32, name="page_max", tag="page_max", align_bytes=64)
-        for g in range(PAGES):
-            nc.vector.tensor_reduce(out=page_max[:, g : g + 1], in_=scores[g][:], axis=mybir.AxisListType.X, op=ALU.max)
-        neg_max = sb.tile([P, 1], F32, name="neg_max")
-        nc.vector.tensor_reduce(out=neg_max[:], in_=page_max[:], axis=mybir.AxisListType.X, op=ALU.max, negate=True)
-
-        vb_early = sb.tile([P, 2 * DV], U8, name="vb_early", tag="page_max", align_bytes=64)
-        nc.vector.tensor_copy(vb_early[:], vb_pool[:].indirect(v_list[:, : 2 * vc]))
-
+        neg_page = sb.tile([P, PAGES], F32, name="neg_page")
         sums = sb.tile([P, PAGES], F32, name="sums")
+        p = []
+        for g in range(PAGES):
+            nc.vector.tensor_reduce(out=neg_page[:, g : g + 1], in_=scores[g][:], axis=mybir.AxisListType.X, op=ALU.max, negate=True)
+            pg = sb.tile([P, PAGES * DV], F32, name=f"p{g}", tag=f"p{g}", align_bytes=64)
+            nc.scalar.activation(out=pg[:, :PAGE], in_=scores[g][:], func=ACT.Exp, bias=neg_page[:, g : g + 1], scale=1.0, accum_out=sums[:, g : g + 1])
+            p.append(pg)
+        neg_max = sb.tile([P, 1], F32, name="neg_max")
+        nc.vector.tensor_reduce(out=neg_max[:], in_=neg_page[:], axis=mybir.AxisListType.X, op=ALU.min)
+        lift = sb.tile([P, PAGES], F32, name="lift")
+        nc.scalar.activation(out=lift[:], in_=neg_page[:], func=ACT.Exp, bias=neg_max[:], scale=-1.0)
+
         w_bf = []
         for g in range(PAGES):
-            p = sb.tile([P, PAGE], F32, name=f"p{g}", tag=f"p{g}", align_bytes=64)
-            nc.scalar.activation(out=p[:], in_=scores[g][:], func=ACT.Exp, bias=neg_max[:], scale=1.0, accum_out=sums[:, g : g + 1])
             w = sb.tile([P, PAGE], F32, name=f"w{g}", align_bytes=64)
-            nc.vector.tensor_tensor(w[:], ts_pool[:].indirect(k_list[:, g * kc : (g + 1) * kc]), p[:], ALU.mult)
+            nc.vector.tensor_tensor(w[:], ts_pool[:].indirect(k_list[:, g * kc : (g + 1) * kc]), p[g][:, :PAGE], ALU.mult)
             pairs = sb.tile([P, 2, P, 2], BF16, name=f"pairs{g}", align_bytes=64)
-            nc.scalar.copy(out=pairs[:], in_=w[:].rearrange("q (s u e) -> q u s e", u=2, e=2))
+            nc.scalar.activation(out=pairs[:], in_=w[:].rearrange("q (s u e) -> q u s e", u=2, e=2), func=ACT.Copy, scale=lift[:, g : g + 1])
             pair_words = pairs[:].rearrange("q u s e -> q (u s e)").bitcast(F32)
             turned = ps.tile([P, 2, NQ], F32, name=f"turned{g}", tag=f"turn{g}")
             for u in range(2):
                 nc.tensor.transpose(turned[:, u, :], pair_words[:, u * P : (u + 1) * P], ident[:])
-            wb = sb.tile([P, NQ * PACK], BF16, name=f"w_bf{g}", tag=f"w_bf{g}", align_bytes=64)
+            wb = sb.tile([P, NQ * PACK], BF16, name=f"w_bf{g}", align_bytes=64)
             nc.scalar.copy(out=wb[:].bitcast(F32).rearrange("s (q u) -> s q u", u=2), in_=turned[:].rearrange("s u q -> s q u"))
             w_bf.append(wb)
 
-        v_early = sb.tile([P, 2 * DV], U32, name="v_early", tag="p2", align_bytes=64)
-        nc.vector.tensor_copy(v_early[:], v_pool[:].bitcast(U32).indirect(v_list[:, : 2 * vc]))
+        v_codes = sb.tile([P, PAGES * DV], U32, name="v_codes", tag="p1", align_bytes=64)
+        nc.vector.tensor_copy(v_codes[:], v_pool[:].bitcast(U32).indirect(v_list[:]))
 
-        w_codes = [sb.tile([P, NQ], U32, name=f"w_codes{g}", align_bytes=64) for g in range(PAGES)]
-        w_bytes = [sb.tile([P, NQ], U8, name=f"w_bytes{g}", align_bytes=64) for g in range(PAGES)]
-
-        def quantise(g):
-            nc.vector.quantize_mx(out=w_codes[g][:].bitcast(FP8X4), scales=w_bytes[g][:], in_=w_bf[g][:])
+        total = sb.tile([P, 1], F32, name="total")
+        inv = sb.tile([P, 1], F32, name="inv")
+        lifted = sb.tile([P, PAGES], F32, name="lifted")
+        nc.vector.scalar_tensor_tensor(out=lifted[:], in0=sums[:], scalar=1.0, in1=lift[:], op0=ALU.mult, op1=ALU.mult, accum_out=total[:])
+        nc.vector.reciprocal(inv[:], total[:])
 
         half = DV // 2
         acc = [ps.tile([P, half], F32, name=f"acc{h}", tag=("acc", "turn3")[h]) for h in range(2)]
-
-        def product(g, codes, scale_bytes):
+        for g in range(PAGES):
+            w_codes = sb.tile([P, NQ], U32, name=f"w_codes{g}", align_bytes=64)
+            w_bytes = sb.tile([P, NQ], U8, name=f"w_bytes{g}", align_bytes=64)
+            nc.vector.quantize_mx(out=w_codes[:].bitcast(FP8X4), scales=w_bytes[:], in_=w_bf[g][:])
             for h in range(2):
+                cols = slice(g * DV + h * half, g * DV + (h + 1) * half)
                 nc.tensor.matmul_mx(
-                    out=acc[h][:], lhsT=w_codes[g][:].bitcast(FP8X4), lhsT_scale=w_bytes[g][:],
-                    rhs=codes[:, h * half : (h + 1) * half].bitcast(FP8X4), rhs_scale=scale_bytes[:, h * half : (h + 1) * half],
+                    out=acc[h][:], lhsT=w_codes[:].bitcast(FP8X4), lhsT_scale=w_bytes[:],
+                    rhs=v_codes[:, cols].bitcast(FP8X4), rhs_scale=v_bytes[VROW:P, cols],
                     start=(g == 0), stop=(g == PAGES - 1),
                 )
-
-        quantise(0)
-        product(0, v_early[:, :DV], vb_early[:, :DV])
-        quantise(1)
-        product(1, v_early[:, DV:], vb_early[:, DV:])
-        total = sb.tile([P, 1], F32, name="total")
-        inv = sb.tile([P, 1], F32, name="inv")
-        sums_again = sb.tile([P, PAGES], F32, name="sums_again")
-        nc.scalar.activation(out=sums_again[:], in_=sums[:], func=ACT.Identity, accum_out=total[:])
-        nc.vector.reciprocal(inv[:], total[:])
-        vb_last = sb.tile([P, DV], U8, name="vb_last", tag="w_bf0", align_bytes=64)
-        nc.vector.tensor_copy(vb_last[:], vb_pool[:].indirect(v_list[:, 2 * vc :]))
-        v_last = sb.tile([P, DV], U32, name="v_last", tag="w_bf1", align_bytes=64)
-        nc.vector.tensor_copy(v_last[:], v_pool[:].bitcast(U32).indirect(v_list[:, 2 * vc :]))
-        quantise(2)
-        product(2, v_last[:], vb_last[:])
         y0 = sb.tile([P, half], F32, name="y0")
         y1 = sb.tile([P, half], F32, name="y1")
         nc.scalar.activation(out=y0[:], in_=acc[0][:], func=ACT.Copy, scale=inv[:])

@@ -20,7 +20,7 @@ PAGE = 512
 PAGES = 3
 POOL_PAGES = 8
 PACK = 4
-VROW = 4
+TOP = 112
 FLOPS = 301989888
 
 
@@ -38,40 +38,33 @@ def tile_attend_pkv8_qpk_kernel(tc, q_words, q_scales, k_words, k_scales, v_word
         ident = sb.tile([P, P], F32, name="ident", align_bytes=64)
         warm2 = sb.tile([P, 1], F32, name="warm2")
 
-        at_qb = 4 * T
-        at_qc = at_qb + NQ
-        at_vb = at_qc + 4 * NQ
-        at_ks = at_vb + POOL_PAGES * DV
-        ks_pool = laid.tile([P, T], U8, name="ks_pool", align_bytes=64, offset=at_ks)
-        ones = laid.tile([P, P], F32, name="ones", align_bytes=64, offset=at_qb - 64)
-        warm = laid.tile([P, 1], F32, name="warm", align_bytes=64, offset=at_vb)
-
-        nc.gpsimd.memset(ks_pool[:, : T // 2].bitcast(I32), 0)
-        nc.vector.memset(ks_pool[:, T // 2 :].bitcast(I32), 0)
-        nc.vector.memset(ones[:], 1.0)
-        nc.vector.memset(warm[:], 0.0)
-        nc.scalar.activation(out=warm2[:], in_=warm[:], func=ACT.Exp)
-        nc.gpsimd.affine_select(out=ident[:], in_=ones[:], pattern=[[-1, P]], compare_op=ALU.is_equal, fill=0.0, base=0, channel_multiplier=1)
-
-        k_rows = k_words[0].rearrange("p t r -> p (t r)").bitcast(I32)
-        nc.sync.dma_start(k_list[:], offs)
-        nc.sync.dma_start(v_list[:], voffs)
-        nc.sync.dma_start(out=ts_cols[:], in_=vs[0].rearrange("(p c) -> p c", p=P))
-        for r in range(4):
-            nc.sync.dma_start(out=ks_pool[r:P:32, :].bitcast(I32), in_=k_scales[0, r:16:4, :].bitcast(I32))
-        k_pool = laid.tile([P, T], I32, name="k_pool", align_bytes=64, offset=0)
-        nc.sync.dma_start(out=k_pool[:], in_=k_rows)
+        ks_pool = laid.tile([P, T], U8, name="ks_pool", align_bytes=64, offset=0)
         vb_pool = sb.tile([P, POOL_PAGES * DV], U8, name="vb_pool", align_bytes=64)
-        nc.vector.memset(vb_pool[:].bitcast(I32), 0)
-        for r in range(4):
-            nc.scalar.dma_start(
-                out=vb_pool[VROW + r : P : 32, :].bitcast(I32).rearrange("p (u e) -> p u e", u=POOL_PAGES),
-                in_=v_scales[:, r:16:4, :].rearrange("u f e -> f u e").bitcast(I32),
-            )
-        q_codes = laid.tile([P, NQ], I32, name="q_codes", align_bytes=64, offset=at_qc)
+        q_codes = sb.tile([P, NQ], I32, name="q_codes", align_bytes=64)
+        k_bytes = sb.tile([P, PAGES * PAGE], U8, name="k_bytes", align_bytes=64)
+        v_bytes = sb.tile([P, PAGES * DV], U8, name="v_bytes", align_bytes=64)
+        at_q = 4 * POOL_PAGES * DV
+        at_k = at_q + NQ
+        ones = laid.tile([P, P], F32, name="ones", align_bytes=64, offset=at_q)
+
+        nc.sync.dma_start(k_list[:], offs)
+        nc.sync.dma_start(out=ks_pool[TOP:, :].bitcast(I32), in_=k_scales[0].bitcast(I32))
+        nc.sync.dma_start(v_list[:], voffs)
+        nc.sync.dma_start(
+            out=vb_pool[TOP:, :].bitcast(I32).rearrange("p (u e) -> p u e", u=POOL_PAGES),
+            in_=v_scales.rearrange("u f e -> f u e").bitcast(I32),
+        )
+        nc.sync.dma_start(out=ts_cols[:], in_=vs[0].rearrange("(p c) -> p c", p=P))
         nc.sync.dma_start(out=q_codes[:], in_=q_words[0, 0].rearrange("p q r -> p (q r)").bitcast(I32))
-        q_bytes = laid.tile([P, NQ], U8, name="q_bytes", align_bytes=64, offset=at_qb)
-        nc.gpsimd.memset(q_bytes[:].bitcast(I32), 0)
+
+        nc.vector.memset(ks_pool[:TOP, :].bitcast(I32), 0)
+        nc.vector.memset(vb_pool[:TOP, :].bitcast(I32), 0)
+        nc.gpsimd.memset(ones[:], 1.0)
+        nc.gpsimd.affine_select(out=ident[:], in_=ones[:], pattern=[[-1, P]], compare_op=ALU.is_equal, fill=0.0, base=0, channel_multiplier=1)
+        k_pool = laid.tile([P, T], I32, name="k_pool", align_bytes=64, offset=at_k)
+        nc.scalar.dma_start(out=k_pool[:], in_=k_words[0].rearrange("p t r -> p (t r)").bitcast(I32))
+        nc.scalar.activation(out=warm2[:], in_=ident[:, :1], func=ACT.Exp)
+        q_bytes = laid.tile([P, NQ], U8, name="q_bytes", align_bytes=64, offset=at_q)
         for r in range(4):
             nc.gpsimd.dma_start(out=q_bytes[r:P:32, :].bitcast(I32), in_=q_scales[0, 0, r:16:4, :].bitcast(I32))
 
@@ -84,17 +77,21 @@ def tile_attend_pkv8_qpk_kernel(tc, q_words, q_scales, k_words, k_scales, v_word
                 nc.tensor.transpose(spread[:, c, :], ts_cols[:, col : col + 1].to_broadcast([P, P]), ident[:])
             nc.scalar.activation(out=ts_view[:, b], in_=spread[:].rearrange("p c i -> p i c"), func=ACT.Copy)
 
-        k_bytes = sb.tile([P, PAGES * PAGE], U8, name="k_bytes", align_bytes=64)
-        nc.vector.tensor_copy(k_bytes[:], ks_pool[:].indirect(k_list[:]))
+        k_rows = sb.tile([P, PAGES * PAGE], U8, name="k_rows", align_bytes=64)
+        nc.vector.tensor_copy(k_rows[:], ks_pool[:].indirect(k_list[:]))
+        for r in range(4):
+            nc.sync.dma_start(out=k_bytes[r:P:32, :].bitcast(I32), in_=k_rows[TOP + r : P : 4, :].bitcast(I32))
 
-        v_bytes = sb.tile([P, PAGES * DV], U8, name="v_bytes", align_bytes=64)
-        nc.vector.tensor_copy(v_bytes[:], vb_pool[:].indirect(v_list[:]))
+        v_rows = sb.tile([P, PAGES * DV], U8, name="v_rows", align_bytes=64)
+        nc.vector.tensor_copy(v_rows[:], vb_pool[:].indirect(v_list[:]))
 
-        v_pool = laid.tile([P, POOL_PAGES * DV], I32, name="v_pool", align_bytes=64, offset=at_ks)
+        v_pool = laid.tile([P, POOL_PAGES * DV], I32, name="v_pool", align_bytes=64, offset=0)
         nc.sync.dma_start(
             out=v_pool[:].rearrange("p (u e) -> p u e", u=POOL_PAGES),
             in_=v_words.rearrange("u p e r -> p u (e r)").bitcast(I32),
         )
+        for r in range(4):
+            nc.sync.dma_start(out=v_bytes[r:P:32, :].bitcast(I32), in_=v_rows[TOP + r : P : 4, :].bitcast(I32))
 
         kc = PAGE // 16
         scores = []
@@ -155,7 +152,7 @@ def tile_attend_pkv8_qpk_kernel(tc, q_words, q_scales, k_words, k_scales, v_word
                 cols = slice(g * DV + h * half, g * DV + (h + 1) * half)
                 nc.tensor.matmul_mx(
                     out=acc[h][:], lhsT=w_codes[:].bitcast(FP8X4), lhsT_scale=w_bytes[:],
-                    rhs=v_codes[:, cols].bitcast(FP8X4), rhs_scale=v_bytes[VROW:P, cols],
+                    rhs=v_codes[:, cols].bitcast(FP8X4), rhs_scale=v_bytes[:, cols],
                     start=(g == 0), stop=(g == PAGES - 1),
                 )
         y0 = sb.tile([P, half], F32, name="y0")

@@ -38,31 +38,30 @@ def tile_attend_pkv8_qpk_kernel(tc, q_words, q_scales, k_words, k_scales, v_word
         ident = sb.tile([P, P], F32, name="ident", align_bytes=64)
         warm2 = sb.tile([P, 1], F32, name="warm2")
 
-        ks_pool = laid.tile([P, T], U8, name="ks_pool", align_bytes=64, offset=0)
-        vb_pool = sb.tile([P, POOL_PAGES * DV], U8, name="vb_pool", align_bytes=64)
+        ks_pool = sb.tile([P, T], U8, name="ks_pool", align_bytes=64)
+        vb_pool = laid.tile([P, POOL_PAGES * DV], U8, name="vb_pool", align_bytes=64, offset=0)
+        k_pool = sb.tile([P, T], I32, name="k_pool", align_bytes=64)
         q_codes = sb.tile([P, NQ], I32, name="q_codes", align_bytes=64)
         k_bytes = sb.tile([P, PAGES * PAGE], U8, name="k_bytes", align_bytes=64)
         v_bytes = sb.tile([P, PAGES * DV], U8, name="v_bytes", align_bytes=64)
         at_q = 4 * POOL_PAGES * DV
-        at_k = at_q + NQ
         ones = laid.tile([P, P], F32, name="ones", align_bytes=64, offset=at_q)
 
         nc.sync.dma_start(k_list[:], offs)
         nc.sync.dma_start(out=ks_pool[TOP:, :].bitcast(I32), in_=k_scales[0].bitcast(I32))
         nc.sync.dma_start(v_list[:], voffs)
-        nc.sync.dma_start(
+        nc.sync.dma_start(out=k_pool[:], in_=k_words[0].rearrange("p t r -> p (t r)").bitcast(I32))
+        nc.scalar.dma_start(
             out=vb_pool[TOP:, :].bitcast(I32).rearrange("p (u e) -> p u e", u=POOL_PAGES),
             in_=v_scales.rearrange("u f e -> f u e").bitcast(I32),
         )
-        nc.sync.dma_start(out=ts_cols[:], in_=vs[0].rearrange("(p c) -> p c", p=P))
-        nc.sync.dma_start(out=q_codes[:], in_=q_words[0, 0].rearrange("p q r -> p (q r)").bitcast(I32))
+        nc.scalar.dma_start(out=ts_cols[:], in_=vs[0].rearrange("(p c) -> p c", p=P))
+        nc.scalar.dma_start(out=q_codes[:], in_=q_words[0, 0].rearrange("p q r -> p (q r)").bitcast(I32))
 
         nc.vector.memset(ks_pool[:TOP, :].bitcast(I32), 0)
         nc.vector.memset(vb_pool[:TOP, :].bitcast(I32), 0)
         nc.gpsimd.memset(ones[:], 1.0)
         nc.gpsimd.affine_select(out=ident[:], in_=ones[:], pattern=[[-1, P]], compare_op=ALU.is_equal, fill=0.0, base=0, channel_multiplier=1)
-        k_pool = laid.tile([P, T], I32, name="k_pool", align_bytes=64, offset=at_k)
-        nc.scalar.dma_start(out=k_pool[:], in_=k_words[0].rearrange("p t r -> p (t r)").bitcast(I32))
         nc.scalar.activation(out=warm2[:], in_=ident[:, :1], func=ACT.Exp)
         q_bytes = laid.tile([P, NQ], U8, name="q_bytes", align_bytes=64, offset=at_q)
         for r in range(4):

@@ -21,6 +21,7 @@ PAGES = 3
 POOL_PAGES = 8
 PACK = 4
 TOP = 112
+MID = 48
 FLOPS = 301989888
 
 
@@ -47,19 +48,22 @@ def tile_attend_pkv8_qpk_kernel(tc, q_words, q_scales, k_words, k_scales, v_word
         at_q = 4 * POOL_PAGES * DV
         ones = laid.tile([P, P], F32, name="ones", align_bytes=64, offset=at_q)
 
+        k_dram = k_words[0].rearrange("p t r -> p (t r)").bitcast(I32)
         nc.sync.dma_start(k_list[:], offs)
-        nc.sync.dma_start(out=ks_pool[TOP:, :].bitcast(I32), in_=k_scales[0].bitcast(I32))
+        nc.sync.dma_start(out=k_pool[:, : T // 2], in_=k_dram[:, : T // 2])
         nc.sync.dma_start(v_list[:], voffs)
-        nc.sync.dma_start(out=k_pool[:], in_=k_words[0].rearrange("p t r -> p (t r)").bitcast(I32))
+        nc.sync.dma_start(out=ts_cols[:], in_=vs[0].rearrange("(p c) -> p c", p=P))
+        nc.sync.dma_start(out=k_pool[:, T // 2 :], in_=k_dram[:, T // 2 :])
+        nc.sync.dma_start(out=q_codes[:], in_=q_words[0, 0].rearrange("p q r -> p (q r)").bitcast(I32))
+        nc.scalar.dma_start(out=ks_pool[TOP:, :].bitcast(I32), in_=k_scales[0].bitcast(I32))
         nc.scalar.dma_start(
-            out=vb_pool[TOP:, :].bitcast(I32).rearrange("p (u e) -> p u e", u=POOL_PAGES),
+            out=vb_pool[MID:64, :].bitcast(I32).rearrange("p (u e) -> p u e", u=POOL_PAGES),
             in_=v_scales.rearrange("u f e -> f u e").bitcast(I32),
         )
-        nc.scalar.dma_start(out=ts_cols[:], in_=vs[0].rearrange("(p c) -> p c", p=P))
-        nc.scalar.dma_start(out=q_codes[:], in_=q_words[0, 0].rearrange("p q r -> p (q r)").bitcast(I32))
 
         nc.vector.memset(ks_pool[:TOP, :].bitcast(I32), 0)
-        nc.vector.memset(vb_pool[:TOP, :].bitcast(I32), 0)
+        nc.vector.memset(vb_pool[:MID, :].bitcast(I32), 0)
+        nc.gpsimd.memset(vb_pool[64:, :].bitcast(I32), 0)
         nc.gpsimd.memset(ones[:], 1.0)
         nc.gpsimd.affine_select(out=ident[:], in_=ones[:], pattern=[[-1, P]], compare_op=ALU.is_equal, fill=0.0, base=0, channel_multiplier=1)
         nc.scalar.activation(out=warm2[:], in_=ident[:, :1], func=ACT.Exp)
@@ -90,7 +94,7 @@ def tile_attend_pkv8_qpk_kernel(tc, q_words, q_scales, k_words, k_scales, v_word
             in_=v_words.rearrange("u p e r -> p u (e r)").bitcast(I32),
         )
         for r in range(4):
-            nc.sync.dma_start(out=v_bytes[r:P:32, :].bitcast(I32), in_=v_rows[TOP + r : P : 4, :].bitcast(I32))
+            nc.sync.dma_start(out=v_bytes[r:P:32, :].bitcast(I32), in_=v_rows[MID + r : 64 : 4, :].bitcast(I32))
 
         kc = PAGE // 16
         scores = []
@@ -128,18 +132,12 @@ def tile_attend_pkv8_qpk_kernel(tc, q_words, q_scales, k_words, k_scales, v_word
             turned = ps.tile([P, 2, NQ], F32, name=f"turned{g}", tag=f"turn{g}")
             for u in range(2):
                 nc.tensor.transpose(turned[:, u, :], pair_words[:, u * P : (u + 1) * P], ident[:])
-            wb = sb.tile([P, NQ * PACK], BF16, name=f"w_bf{g}", align_bytes=64)
+            wb = sb.tile([P, NQ * PACK], BF16, name=f"w_bf{g}", tag=f"w_bf{g}", align_bytes=64)
             nc.scalar.copy(out=wb[:].bitcast(F32).rearrange("s (q u) -> s q u", u=2), in_=turned[:].rearrange("s u q -> s q u"))
             w_bf.append(wb)
 
         v_codes = sb.tile([P, PAGES * DV], U32, name="v_codes", tag="p1", align_bytes=64)
         nc.vector.tensor_copy(v_codes[:], v_pool[:].bitcast(U32).indirect(v_list[:]))
-
-        total = sb.tile([P, 1], F32, name="total")
-        inv = sb.tile([P, 1], F32, name="inv")
-        lifted = sb.tile([P, PAGES], F32, name="lifted")
-        nc.vector.scalar_tensor_tensor(out=lifted[:], in0=sums[:], scalar=1.0, in1=lift[:], op0=ALU.mult, op1=ALU.mult, accum_out=total[:])
-        nc.vector.reciprocal(inv[:], total[:])
 
         half = DV // 2
         acc = [ps.tile([P, half], F32, name=f"acc{h}", tag=("acc", "turn3")[h]) for h in range(2)]
@@ -154,6 +152,12 @@ def tile_attend_pkv8_qpk_kernel(tc, q_words, q_scales, k_words, k_scales, v_word
                     rhs=v_codes[:, cols].bitcast(FP8X4), rhs_scale=v_bytes[:, cols],
                     start=(g == 0), stop=(g == PAGES - 1),
                 )
+        total = sb.tile([P, 1], F32, name="total")
+        inv = sb.tile([P, 1], F32, name="inv")
+        lifted = sb.tile([P, PAGES], F32, name="lifted", tag="w_bf2", align_bytes=64)
+        nc.vector.scalar_tensor_tensor(out=lifted[:], in0=sums[:], scalar=1.0, in1=lift[:], op0=ALU.mult, op1=ALU.mult, accum_out=total[:])
+        nc.vector.reciprocal(inv[:], total[:])
+
         y0 = sb.tile([P, half], F32, name="y0")
         y1 = sb.tile([P, half], F32, name="y1")
         nc.scalar.activation(out=y0[:], in_=acc[0][:], func=ACT.Copy, scale=inv[:])

@@ -45,31 +45,38 @@ def tile_attend_pkv8_qpk_kernel(tc, q_words, q_scales, k_words, k_scales, v_word
         q_codes = sb.tile([P, NQ], I32, name="q_codes", align_bytes=64)
         k_bytes = sb.tile([P, PAGES * PAGE], U8, name="k_bytes", align_bytes=64)
         v_bytes = sb.tile([P, PAGES * DV], U8, name="v_bytes", align_bytes=64)
-        at_q = 4 * POOL_PAGES * DV
-        ones = laid.tile([P, P], F32, name="ones", align_bytes=64, offset=at_q)
+        q_bytes = sb.tile([P, NQ], U8, name="q_bytes", align_bytes=64)
+        ones = sb.tile([P, P], F32, name="ones", align_bytes=64)
 
         k_dram = k_words[0].rearrange("p t r -> p (t r)").bitcast(I32)
+        nc.sync.dma_start(out=ks_pool[TOP:, :].bitcast(I32), in_=k_scales[0].bitcast(I32))
         nc.sync.dma_start(k_list[:], offs)
         nc.sync.dma_start(out=k_pool[:, : T // 2], in_=k_dram[:, : T // 2])
         nc.sync.dma_start(v_list[:], voffs)
-        nc.sync.dma_start(out=ts_cols[:], in_=vs[0].rearrange("(p c) -> p c", p=P))
         nc.sync.dma_start(out=k_pool[:, T // 2 :], in_=k_dram[:, T // 2 :])
         nc.sync.dma_start(out=q_codes[:], in_=q_words[0, 0].rearrange("p q r -> p (q r)").bitcast(I32))
-        nc.scalar.dma_start(out=ks_pool[TOP:, :].bitcast(I32), in_=k_scales[0].bitcast(I32))
+        nc.scalar.dma_start(out=ts_cols[:], in_=vs[0].rearrange("(p c) -> p c", p=P))
         nc.scalar.dma_start(
             out=vb_pool[MID:64, :].bitcast(I32).rearrange("p (u e) -> p u e", u=POOL_PAGES),
             in_=v_scales.rearrange("u f e -> f u e").bitcast(I32),
         )
 
+        def load_q_scales(r):
+            nc.scalar.dma_start(out=q_bytes[r:P:32, :].bitcast(I32), in_=q_scales[0, 0, r:16:4, :].bitcast(I32))
+
+        load_q_scales(0)
+        load_q_scales(1)
+        warm = sb.tile([P, 1], F32, name="warm")
+        nc.gpsimd.memset(warm[:], 0.0)
+        nc.scalar.activation(out=warm2[:], in_=warm[:], func=ACT.Exp)
+        load_q_scales(2)
+        load_q_scales(3)
+
         nc.vector.memset(ks_pool[:TOP, :].bitcast(I32), 0)
         nc.vector.memset(vb_pool[:MID, :].bitcast(I32), 0)
-        nc.gpsimd.memset(vb_pool[64:, :].bitcast(I32), 0)
+        nc.vector.memset(vb_pool[64:, :].bitcast(I32), 0)
         nc.gpsimd.memset(ones[:], 1.0)
         nc.gpsimd.affine_select(out=ident[:], in_=ones[:], pattern=[[-1, P]], compare_op=ALU.is_equal, fill=0.0, base=0, channel_multiplier=1)
-        nc.scalar.activation(out=warm2[:], in_=ident[:, :1], func=ACT.Exp)
-        q_bytes = laid.tile([P, NQ], U8, name="q_bytes", align_bytes=64, offset=at_q)
-        for r in range(4):
-            nc.gpsimd.dma_start(out=q_bytes[r:P:32, :].bitcast(I32), in_=q_scales[0, 0, r:16:4, :].bitcast(I32))
 
         per = T // P
         ts_view = ts_pool[:].rearrange("p (i b c) -> p b i c", b=per // PACK, c=PACK)

@@ -37,7 +37,6 @@ def tile_attend_pkv8_qpk_kernel(tc, q_words, q_scales, k_words, k_scales, v_word
         ts_pool = sb.tile([P, T], F32, name="ts_pool", align_bytes=64)
         ts_cols = sb.tile([P, T // P], F32, name="ts_cols", align_bytes=64)
         ident = sb.tile([P, P], F32, name="ident", align_bytes=64)
-        warm2 = sb.tile([P, 1], F32, name="warm2")
 
         ks_pool = sb.tile([P, T], U8, name="ks_pool", align_bytes=64)
         vb_pool = laid.tile([P, POOL_PAGES * DV], U8, name="vb_pool", align_bytes=64, offset=0)
@@ -66,9 +65,6 @@ def tile_attend_pkv8_qpk_kernel(tc, q_words, q_scales, k_words, k_scales, v_word
 
         load_q_scales(0)
         load_q_scales(1)
-        warm = sb.tile([P, 1], F32, name="warm")
-        nc.gpsimd.memset(warm[:], 0.0)
-        nc.scalar.activation(out=warm2[:], in_=warm[:], func=ACT.Exp)
         load_q_scales(2)
         load_q_scales(3)
 

@@ -117,30 +117,43 @@ def tile_attend_pkv8_qpk_kernel(tc, q_words, q_scales, k_words, k_scales, v_word
         p = []
         for g in range(PAGES):
             nc.vector.tensor_reduce(out=neg_page[:, g : g + 1], in_=scores[g][:], axis=mybir.AxisListType.X, op=ALU.max, negate=True)
-            pg = sb.tile([P, PAGES * DV], F32, name=f"p{g}", tag=f"p{g}", align_bytes=64)
-            nc.scalar.activation(out=pg[:, :PAGE], in_=scores[g][:], func=ACT.Exp, bias=neg_page[:, g : g + 1], scale=1.0, accum_out=sums[:, g : g + 1])
+            pg = sb.tile([P, PAGE], F32, name=f"p{g}", align_bytes=64)
+            nc.scalar.activation(out=pg[:], in_=scores[g][:], func=ACT.Exp, bias=neg_page[:, g : g + 1], scale=1.0, accum_out=sums[:, g : g + 1])
             p.append(pg)
+        def weigh(g):
+            w = sb.tile([P, PAGES * DV], F32, name=f"w{g}", tag=f"w{g}", align_bytes=64)
+            nc.vector.tensor_tensor(w[:, :PAGE], ts_pool[:].indirect(k_list[:, g * kc : (g + 1) * kc]), p[g][:], ALU.mult)
+            return w[:, :PAGE].rearrange("q (s u e) -> q u s e", u=2, e=2)
+
+        dealt = [weigh(0)]
         neg_max = sb.tile([P, 1], F32, name="neg_max")
         nc.vector.tensor_reduce(out=neg_max[:], in_=neg_page[:], axis=mybir.AxisListType.X, op=ALU.min)
         lift = sb.tile([P, PAGES], F32, name="lift")
         nc.scalar.activation(out=lift[:], in_=neg_page[:], func=ACT.Exp, bias=neg_max[:], scale=-1.0)
+        dealt.extend(weigh(g) for g in range(1, PAGES))
 
         w_bf = []
         for g in range(PAGES):
-            w = sb.tile([P, PAGE], F32, name=f"w{g}", align_bytes=64)
-            nc.vector.tensor_tensor(w[:], ts_pool[:].indirect(k_list[:, g * kc : (g + 1) * kc]), p[g][:, :PAGE], ALU.mult)
             pairs = sb.tile([P, 2, P, 2], BF16, name=f"pairs{g}", align_bytes=64)
-            nc.scalar.activation(out=pairs[:], in_=w[:].rearrange("q (s u e) -> q u s e", u=2, e=2), func=ACT.Copy, scale=lift[:, g : g + 1])
+            if g == 0:
+                nc.scalar.activation(out=pairs[:], in_=dealt[g], func=ACT.Copy, scale=lift[:, g : g + 1])
+            else:
+                nc.vector.tensor_scalar(out=pairs[:], in0=dealt[g], scalar1=lift[:, g : g + 1], scalar2=None, op0=ALU.mult)
             pair_words = pairs[:].rearrange("q u s e -> q (u s e)").bitcast(F32)
             turned = ps.tile([P, 2, NQ], F32, name=f"turned{g}", tag=f"turn{g}")
             for u in range(2):
                 nc.tensor.transpose(turned[:, u, :], pair_words[:, u * P : (u + 1) * P], ident[:])
-            wb = sb.tile([P, NQ * PACK], BF16, name=f"w_bf{g}", tag=f"w_bf{g}", align_bytes=64)
+            wb = sb.tile([P, NQ * PACK], BF16, name=f"w_bf{g}", align_bytes=64)
             nc.scalar.copy(out=wb[:].bitcast(F32).rearrange("s (q u) -> s q u", u=2), in_=turned[:].rearrange("s u q -> s q u"))
             w_bf.append(wb)
 
-        v_codes = sb.tile([P, PAGES * DV], U32, name="v_codes", tag="p1", align_bytes=64)
+        total = sb.tile([P, 1], F32, name="total")
+        inv = sb.tile([P, 1], F32, name="inv")
+        lifted = sb.tile([P, PAGES], F32, name="lifted")
+        nc.vector.scalar_tensor_tensor(out=lifted[:], in0=sums[:], scalar=1.0, in1=lift[:], op0=ALU.mult, op1=ALU.mult, accum_out=total[:])
+        v_codes = sb.tile([P, PAGES * DV], U32, name="v_codes", tag="w1", align_bytes=64)
         nc.vector.tensor_copy(v_codes[:], v_pool[:].bitcast(U32).indirect(v_list[:]))
+        nc.vector.reciprocal(inv[:], total[:])
 
         half = DV // 2
         acc = [ps.tile([P, half], F32, name=f"acc{h}", tag=("acc", "turn3")[h]) for h in range(2)]
@@ -155,11 +168,6 @@ def tile_attend_pkv8_qpk_kernel(tc, q_words, q_scales, k_words, k_scales, v_word
                     rhs=v_codes[:, cols].bitcast(FP8X4), rhs_scale=v_bytes[:, cols],
                     start=(g == 0), stop=(g == PAGES - 1),
                 )
-        total = sb.tile([P, 1], F32, name="total")
-        inv = sb.tile([P, 1], F32, name="inv")
-        lifted = sb.tile([P, PAGES], F32, name="lifted", tag="w_bf2", align_bytes=64)
-        nc.vector.scalar_tensor_tensor(out=lifted[:], in0=sums[:], scalar=1.0, in1=lift[:], op0=ALU.mult, op1=ALU.mult, accum_out=total[:])
-        nc.vector.reciprocal(inv[:], total[:])
 
         y0 = sb.tile([P, half], F32, name="y0")
         y1 = sb.tile([P, half], F32, name="y1")

@@ -22,6 +22,7 @@ POOL_PAGES = 8
 PACK = 4
 TOP = 112
 MID = 48
+SPREAD = 3 * T // 4
 FLOPS = 301989888
 
 
@@ -34,11 +35,10 @@ def tile_attend_pkv8_qpk_kernel(tc, q_words, q_scales, k_words, k_scales, v_word
 
         k_list = sb.tile([P, PAGES * PAGE // 16], U16, name="k_list")
         v_list = sb.tile([P, PAGES * DV // 16], U16, name="v_list")
-        ts_pool = sb.tile([P, T], F32, name="ts_pool", align_bytes=64)
-        ts_cols = sb.tile([P, T // P], F32, name="ts_cols", align_bytes=64)
+        ts_cols = sb.tile([P, SPREAD // P], F32, name="ts_cols", align_bytes=64)
         ident = sb.tile([P, P], F32, name="ident", align_bytes=64)
 
-        ks_pool = sb.tile([P, T], U8, name="ks_pool", align_bytes=64)
+        ks_pool = sb.tile([P, T], U8, name="ks_pool", tag="ts_pool", align_bytes=64)
         vb_pool = laid.tile([P, POOL_PAGES * DV], U8, name="vb_pool", align_bytes=64, offset=0)
         k_pool = sb.tile([P, T], I32, name="k_pool", align_bytes=64)
         q_codes = sb.tile([P, NQ], I32, name="q_codes", align_bytes=64)
@@ -47,26 +47,24 @@ def tile_attend_pkv8_qpk_kernel(tc, q_words, q_scales, k_words, k_scales, v_word
         q_bytes = sb.tile([P, NQ], U8, name="q_bytes", align_bytes=64)
         ones = sb.tile([P, P], F32, name="ones", align_bytes=64)
 
+        def load_q_scales(queue, r):
+            queue.dma_start(out=q_bytes[r:P:32, :].bitcast(I32), in_=q_scales[0, 0, r:16:4, :].bitcast(I32))
+
         k_dram = k_words[0].rearrange("p t r -> p (t r)").bitcast(I32)
         nc.sync.dma_start(out=ks_pool[TOP:, :].bitcast(I32), in_=k_scales[0].bitcast(I32))
         nc.sync.dma_start(k_list[:], offs)
         nc.sync.dma_start(out=k_pool[:, : T // 2], in_=k_dram[:, : T // 2])
         nc.sync.dma_start(v_list[:], voffs)
+        load_q_scales(nc.sync, 3)
         nc.sync.dma_start(out=k_pool[:, T // 2 :], in_=k_dram[:, T // 2 :])
         nc.sync.dma_start(out=q_codes[:], in_=q_words[0, 0].rearrange("p q r -> p (q r)").bitcast(I32))
-        nc.scalar.dma_start(out=ts_cols[:], in_=vs[0].rearrange("(p c) -> p c", p=P))
+        nc.scalar.dma_start(out=ts_cols[:], in_=vs[0, :SPREAD].rearrange("(p c) -> p c", p=P))
         nc.scalar.dma_start(
             out=vb_pool[MID:64, :].bitcast(I32).rearrange("p (u e) -> p u e", u=POOL_PAGES),
             in_=v_scales.rearrange("u f e -> f u e").bitcast(I32),
         )
-
-        def load_q_scales(r):
-            nc.scalar.dma_start(out=q_bytes[r:P:32, :].bitcast(I32), in_=q_scales[0, 0, r:16:4, :].bitcast(I32))
-
-        load_q_scales(0)
-        load_q_scales(1)
-        load_q_scales(2)
-        load_q_scales(3)
+        for r in range(3):
+            load_q_scales(nc.scalar, r)
 
         nc.vector.memset(ks_pool[:TOP, :].bitcast(I32), 0)
         nc.vector.memset(vb_pool[:MID, :].bitcast(I32), 0)
@@ -74,19 +72,21 @@ def tile_attend_pkv8_qpk_kernel(tc, q_words, q_scales, k_words, k_scales, v_word
         nc.gpsimd.memset(ones[:], 1.0)
         nc.gpsimd.affine_select(out=ident[:], in_=ones[:], pattern=[[-1, P]], compare_op=ALU.is_equal, fill=0.0, base=0, channel_multiplier=1)
 
-        per = T // P
-        ts_view = ts_pool[:].rearrange("p (i b c) -> p b i c", b=per // PACK, c=PACK)
+        k_rows = sb.tile([P, PAGES * PAGE], U8, name="k_rows", align_bytes=64)
+        nc.vector.tensor_copy(k_rows[:], ks_pool[:].indirect(k_list[:]))
+        for r in range(4):
+            nc.sync.dma_start(out=k_bytes[r:P:32, :].bitcast(I32), in_=k_rows[TOP + r : P : 4, :].bitcast(I32))
+
+        ts_pool = sb.tile([P, T], F32, name="ts_pool", tag="ts_pool", align_bytes=64)
+        nc.sync.dma_start(out=ts_pool[:, SPREAD:], in_=vs[:, SPREAD:])
+        per = SPREAD // P
+        ts_view = ts_pool[:, :SPREAD].rearrange("p (i b c) -> p b i c", b=per // PACK, c=PACK)
         for b in range(per // PACK):
             spread = ps.tile([P, PACK, P], F32, name=f"spread{b}", tag=f"turn{b % 4}")
             for c in range(PACK):
                 col = PACK * b + c
                 nc.tensor.transpose(spread[:, c, :], ts_cols[:, col : col + 1].to_broadcast([P, P]), ident[:])
             nc.scalar.activation(out=ts_view[:, b], in_=spread[:].rearrange("p c i -> p i c"), func=ACT.Copy)
-
-        k_rows = sb.tile([P, PAGES * PAGE], U8, name="k_rows", align_bytes=64)
-        nc.vector.tensor_copy(k_rows[:], ks_pool[:].indirect(k_list[:]))
-        for r in range(4):
-            nc.sync.dma_start(out=k_bytes[r:P:32, :].bitcast(I32), in_=k_rows[TOP + r : P : 4, :].bitcast(I32))
 
         v_rows = sb.tile([P, PAGES * DV], U8, name="v_rows", align_bytes=64)
         nc.vector.tensor_copy(v_rows[:], vb_pool[:].indirect(v_list[:]))
@@ -117,7 +117,7 @@ def tile_attend_pkv8_qpk_kernel(tc, q_words, q_scales, k_words, k_scales, v_word
         p = []
         for g in range(PAGES):
             nc.vector.tensor_reduce(out=neg_page[:, g : g + 1], in_=scores[g][:], axis=mybir.AxisListType.X, op=ALU.max, negate=True)
-            pg = sb.tile([P, PAGE], F32, name=f"p{g}", align_bytes=64)
+            pg = sb.tile([P, PAGE], F32, name=f"p{g}", tag=f"p{g}", align_bytes=64)
             nc.scalar.activation(out=pg[:], in_=scores[g][:], func=ACT.Exp, bias=neg_page[:, g : g + 1], scale=1.0, accum_out=sums[:, g : g + 1])
             p.append(pg)
         def weigh(g):
@@ -149,7 +149,7 @@ def tile_attend_pkv8_qpk_kernel(tc, q_words, q_scales, k_words, k_scales, v_word
 
         total = sb.tile([P, 1], F32, name="total")
         inv = sb.tile([P, 1], F32, name="inv")
-        lifted = sb.tile([P, PAGES], F32, name="lifted")
+        lifted = sb.tile([P, PAGES], F32, name="lifted", tag="p2", align_bytes=64)
         nc.vector.scalar_tensor_tensor(out=lifted[:], in0=sums[:], scalar=1.0, in1=lift[:], op0=ALU.mult, op1=ALU.mult, accum_out=total[:])
         v_codes = sb.tile([P, PAGES * DV], U32, name="v_codes", tag="w1", align_bytes=64)
         nc.vector.tensor_copy(v_codes[:], v_pool[:].bitcast(U32).indirect(v_list[:]))

@@ -11,18 +11,23 @@ U8 = mybir.dt.uint8
 FP8X4 = mybir.dt.float8_e4m3fn_x4
 ALU = mybir.AluOpType
 ACT = mybir.ActivationFunctionType
+ALONG_FREE = mybir.AxisListType.X
 
 P = 128
 T = 4096
 NQ = 128
 DV = 256
 PAGE = 512
+HALF = PAGE // 2
 PAGES = 3
 POOL_PAGES = 8
 PACK = 4
-TOP = 112
-MID = 48
-SPREAD = 3 * T // 4
+LIST_ROWS = 16
+K_ROW = 112
+V_ROW = 48
+EXP_HEAD = 96
+WEIGH_HEAD = 320
+P_LAST_AT = POOL_PAGES * DV * 4
 FLOPS = 301989888
 
 
@@ -33,145 +38,170 @@ def tile_attend_pkv8_qpk_kernel(tc, q_words, q_scales, k_words, k_scales, v_word
         laid = ctx.enter_context(tc.tile_pool(name="laid", bufs=1))
         ps = ctx.enter_context(tc.psum_pool(name="ps", bufs=1))
 
-        k_list = sb.tile([P, PAGES * PAGE // 16], U16, name="k_list")
-        v_list = sb.tile([P, PAGES * DV // 16], U16, name="v_list")
-        ts_cols = sb.tile([P, SPREAD // P], F32, name="ts_cols", align_bytes=64)
+        k_list = sb.tile([P, PAGES * PAGE // LIST_ROWS], U16, name="k_list")
+        v_list = sb.tile([P, PAGES * DV // LIST_ROWS], U16, name="v_list")
+        k_pool = sb.tile([P, T], I32, name="k_pool", align_bytes=64)
+        k_scale_pool = sb.tile([P, T], U8, name="k_scale_pool", align_bytes=64)
+        v_scale_pool = laid.tile([P, POOL_PAGES * DV], U8, name="v_scale_pool", align_bytes=64, offset=0)
+        vs_pool = sb.tile([P, T], F32, name="vs_pool", align_bytes=64)
+        vs_cols = sb.tile([P, T // P], F32, name="vs_cols", align_bytes=64)
+        q_codes = sb.tile([P, NQ], I32, name="q_codes", align_bytes=64)
+        q_plane = sb.tile([P, NQ], U8, name="q_plane", align_bytes=64)
+        k_plane = sb.tile([P, PAGES * PAGE], U8, name="k_plane", align_bytes=64)
+        v_plane = sb.tile([P, PAGES * DV], U8, name="v_plane", align_bytes=64)
+        ones = sb.tile([P, P], F32, name="ones", align_bytes=64)
         ident = sb.tile([P, P], F32, name="ident", align_bytes=64)
 
-        ks_pool = sb.tile([P, T], U8, name="ks_pool", tag="ts_pool", align_bytes=64)
-        vb_pool = laid.tile([P, POOL_PAGES * DV], U8, name="vb_pool", align_bytes=64, offset=0)
-        k_pool = sb.tile([P, T], I32, name="k_pool", align_bytes=64)
-        q_codes = sb.tile([P, NQ], I32, name="q_codes", align_bytes=64)
-        k_bytes = sb.tile([P, PAGES * PAGE], U8, name="k_bytes", align_bytes=64)
-        v_bytes = sb.tile([P, PAGES * DV], U8, name="v_bytes", align_bytes=64)
-        q_bytes = sb.tile([P, NQ], U8, name="q_bytes", align_bytes=64)
-        ones = sb.tile([P, P], F32, name="ones", align_bytes=64)
-
-        def load_q_scales(queue, r):
-            queue.dma_start(out=q_bytes[r:P:32, :].bitcast(I32), in_=q_scales[0, 0, r:16:4, :].bitcast(I32))
-
         k_dram = k_words[0].rearrange("p t r -> p (t r)").bitcast(I32)
-        nc.sync.dma_start(out=ks_pool[TOP:, :].bitcast(I32), in_=k_scales[0].bitcast(I32))
+        nc.sync.dma_start(out=k_scale_pool[K_ROW:, :].bitcast(I32), in_=k_scales[0].bitcast(I32))
         nc.sync.dma_start(k_list[:], offs)
         nc.sync.dma_start(out=k_pool[:, : T // 2], in_=k_dram[:, : T // 2])
         nc.sync.dma_start(v_list[:], voffs)
-        load_q_scales(nc.sync, 3)
         nc.sync.dma_start(out=k_pool[:, T // 2 :], in_=k_dram[:, T // 2 :])
         nc.sync.dma_start(out=q_codes[:], in_=q_words[0, 0].rearrange("p q r -> p (q r)").bitcast(I32))
-        nc.scalar.dma_start(out=ts_cols[:], in_=vs[0, :SPREAD].rearrange("(p c) -> p c", p=P))
+        nc.scalar.dma_start(out=vs_cols[:], in_=vs[0].rearrange("(p c) -> p c", p=P))
         nc.scalar.dma_start(
-            out=vb_pool[MID:64, :].bitcast(I32).rearrange("p (u e) -> p u e", u=POOL_PAGES),
+            out=v_scale_pool[V_ROW:64, :].bitcast(I32).rearrange("p (u e) -> p u e", u=POOL_PAGES),
             in_=v_scales.rearrange("u f e -> f u e").bitcast(I32),
         )
-        for r in range(3):
-            load_q_scales(nc.scalar, r)
+        for r in range(4):
+            nc.scalar.dma_start(out=q_plane[r:P:32, :].bitcast(I32), in_=q_scales[0, 0, r:16:4, :].bitcast(I32))
 
-        nc.vector.memset(ks_pool[:TOP, :].bitcast(I32), 0)
-        nc.vector.memset(vb_pool[:MID, :].bitcast(I32), 0)
-        nc.vector.memset(vb_pool[64:, :].bitcast(I32), 0)
+        nc.vector.memset(k_scale_pool[:K_ROW, :].bitcast(I32), 0)
+        nc.vector.memset(v_scale_pool[:V_ROW, :].bitcast(I32), 0)
+        nc.vector.memset(v_scale_pool[64:, :].bitcast(I32), 0)
         nc.gpsimd.memset(ones[:], 1.0)
         nc.gpsimd.affine_select(out=ident[:], in_=ones[:], pattern=[[-1, P]], compare_op=ALU.is_equal, fill=0.0, base=0, channel_multiplier=1)
 
-        k_rows = sb.tile([P, PAGES * PAGE], U8, name="k_rows", align_bytes=64)
-        nc.vector.tensor_copy(k_rows[:], ks_pool[:].indirect(k_list[:]))
-        for r in range(4):
-            nc.sync.dma_start(out=k_bytes[r:P:32, :].bitcast(I32), in_=k_rows[TOP + r : P : 4, :].bitcast(I32))
+        vs_view = vs_pool[:].rearrange("p (page u i j c) -> p u j page i c", page=POOL_PAGES, u=2, i=16, c=PACK)
+        for j in range(4):
+            for u in range(2):
+                spread = ps.tile([P, PACK, P], F32, name=f"spread{j}_{u}", tag=f"turn{(2 * j + u) % 4}")
+                for c in range(PACK):
+                    col = 8 * j + 4 * (c // 2) + 2 * u + c % 2
+                    nc.tensor.transpose(spread[:, c, :], vs_cols[:, col : col + 1].to_broadcast([P, P]), ident[:])
+                nc.scalar.activation(out=vs_view[:, u, j], in_=spread[:].rearrange("p c (page i) -> p page i c", i=16), func=ACT.Copy)
 
-        ts_pool = sb.tile([P, T], F32, name="ts_pool", tag="ts_pool", align_bytes=64)
-        nc.sync.dma_start(out=ts_pool[:, SPREAD:], in_=vs[:, SPREAD:])
-        per = SPREAD // P
-        ts_view = ts_pool[:, :SPREAD].rearrange("p (i b c) -> p b i c", b=per // PACK, c=PACK)
-        for b in range(per // PACK):
-            spread = ps.tile([P, PACK, P], F32, name=f"spread{b}", tag=f"turn{b % 4}")
-            for c in range(PACK):
-                col = PACK * b + c
-                nc.tensor.transpose(spread[:, c, :], ts_cols[:, col : col + 1].to_broadcast([P, P]), ident[:])
-            nc.scalar.activation(out=ts_view[:, b], in_=spread[:].rearrange("p c i -> p i c"), func=ACT.Copy)
+        k_rows = sb.tile([P, PAGES * PAGE], U8, name="k_rows", align_bytes=64)
+        nc.vector.tensor_copy(k_rows[:], k_scale_pool[:].indirect(k_list[:]))
+        for r in range(4):
+            nc.sync.dma_start(out=k_plane[r:P:32, :].bitcast(I32), in_=k_rows[K_ROW + r : P : 4, :].bitcast(I32))
 
         v_rows = sb.tile([P, PAGES * DV], U8, name="v_rows", align_bytes=64)
-        nc.vector.tensor_copy(v_rows[:], vb_pool[:].indirect(v_list[:]))
-
+        nc.vector.tensor_copy(v_rows[:], v_scale_pool[:].indirect(v_list[:]))
         v_pool = laid.tile([P, POOL_PAGES * DV], I32, name="v_pool", align_bytes=64, offset=0)
         nc.sync.dma_start(
             out=v_pool[:].rearrange("p (u e) -> p u e", u=POOL_PAGES),
             in_=v_words.rearrange("u p e r -> p u (e r)").bitcast(I32),
         )
         for r in range(4):
-            nc.sync.dma_start(out=v_bytes[r:P:32, :].bitcast(I32), in_=v_rows[MID + r : 64 : 4, :].bitcast(I32))
+            nc.sync.dma_start(out=v_plane[r:P:32, :].bitcast(I32), in_=v_rows[V_ROW + r : 64 : 4, :].bitcast(I32))
 
-        kc = PAGE // 16
+        def k_offsets(g, a, b):
+            return k_list[:, (g * PAGE + a) // LIST_ROWS : (g * PAGE + b) // LIST_ROWS]
+
         scores = []
         for g in range(PAGES):
             k_codes = sb.tile([P, PAGE], U32, name=f"k_codes{g}", align_bytes=64)
-            nc.vector.tensor_copy(k_codes[:], k_pool[:].bitcast(U32).indirect(k_list[:, g * kc : (g + 1) * kc]))
+            nc.vector.tensor_copy(k_codes[:], k_pool[:].bitcast(U32).indirect(k_offsets(g, 0, PAGE)))
             bank = ps.tile([P, PAGE], F32, name=f"score{g}")
             nc.tensor.matmul_mx(
-                out=bank[:], lhsT=q_codes[:].bitcast(FP8X4), lhsT_scale=q_bytes[:],
-                rhs=k_codes[:].bitcast(FP8X4), rhs_scale=k_bytes[:, g * PAGE : (g + 1) * PAGE],
+                out=bank[:], lhsT=q_codes[:].bitcast(FP8X4), lhsT_scale=q_plane[:],
+                rhs=k_codes[:].bitcast(FP8X4), rhs_scale=k_plane[:, g * PAGE : (g + 1) * PAGE],
                 start=True, stop=True,
             )
-            scores.append(bank)
+            scores.append(bank[:])
 
+        last = PAGES - 1
         neg_page = sb.tile([P, PAGES], F32, name="neg_page")
-        sums = sb.tile([P, PAGES], F32, name="sums")
-        p = []
-        for g in range(PAGES):
-            nc.vector.tensor_reduce(out=neg_page[:, g : g + 1], in_=scores[g][:], axis=mybir.AxisListType.X, op=ALU.max, negate=True)
-            pg = sb.tile([P, PAGE], F32, name=f"p{g}", tag=f"p{g}", align_bytes=64)
-            nc.scalar.activation(out=pg[:], in_=scores[g][:], func=ACT.Exp, bias=neg_page[:, g : g + 1], scale=1.0, accum_out=sums[:, g : g + 1])
-            p.append(pg)
-        def weigh(g):
-            w = sb.tile([P, PAGES * DV], F32, name=f"w{g}", tag=f"w{g}", align_bytes=64)
-            nc.vector.tensor_tensor(w[:, :PAGE], ts_pool[:].indirect(k_list[:, g * kc : (g + 1) * kc]), p[g][:], ALU.mult)
-            return w[:, :PAGE].rearrange("q (s u e) -> q u s e", u=2, e=2)
+        sums = sb.tile([P, PAGES + 1], F32, name="sums")
+        p = [sb.tile([P, PAGE], F32, name=f"p{g}", align_bytes=64) for g in range(last)]
+        p.append(laid.tile([P, PAGE], F32, name="p_last", align_bytes=64, offset=P_LAST_AT))
+        w = [sb.tile([P, PAGE], F32, name=f"w{g}", align_bytes=64) for g in range(PAGES)]
 
-        dealt = [weigh(0)]
+        def exp_part(g, a, b, col):
+            nc.scalar.activation(
+                out=p[g][:].rearrange("q (u s e) -> q u s e", u=2, e=2)[:, :, a:b], in_=scores[g].rearrange("q (s u e) -> q u s e", u=2, e=2)[:, :, a:b],
+                func=ACT.Exp, bias=neg_page[:, g : g + 1], scale=1.0, accum_out=sums[:, col : col + 1],
+            )
+
+        def weigh(g, a, b):
+            nc.vector.tensor_tensor(w[g][:, a:b], vs_pool[:].indirect(k_offsets(g, a, b)), p[g][:, a:b], ALU.mult)
+
+        for g in range(PAGES):
+            nc.vector.tensor_reduce(out=neg_page[:, g : g + 1], in_=scores[g], axis=ALONG_FREE, op=ALU.max, negate=True)
+            exp_part(g, 0, P if g < last else EXP_HEAD, g)
+
+        weigh(0, 0, WEIGH_HEAD)
         neg_max = sb.tile([P, 1], F32, name="neg_max")
-        nc.vector.tensor_reduce(out=neg_max[:], in_=neg_page[:], axis=mybir.AxisListType.X, op=ALU.min)
+        nc.vector.tensor_reduce(out=neg_max[:], in_=neg_page[:], axis=ALONG_FREE, op=ALU.min)
         lift = sb.tile([P, PAGES], F32, name="lift")
         nc.scalar.activation(out=lift[:], in_=neg_page[:], func=ACT.Exp, bias=neg_max[:], scale=-1.0)
-        dealt.extend(weigh(g) for g in range(1, PAGES))
+        exp_part(last, EXP_HEAD, P, PAGES)
+        weigh(0, WEIGH_HEAD, PAGE)
+        weigh(1, 0, PAGE)
+        last_cuts = (0, HALF, HALF + P, PAGE)
+        for a, b in zip(last_cuts, last_cuts[1:]):
+            weigh(last, a, b)
 
+        pairs = [[sb.tile([P, HALF], BF16, name=f"pairs{g}_{u}", align_bytes=64) for u in range(2)] for g in range(PAGES)]
+        turned = [ps.tile([P, 2, NQ], F32, name=f"turned{g}", tag=f"turn{g}") for g in range(PAGES)]
+
+        def pairs_part(g, a, b):
+            u = a // HALF
+            return pairs[g][u][:, a - u * HALF : b - u * HALF]
+
+        def round_on_scalar(g, a, b):
+            nc.scalar.activation(out=pairs_part(g, a, b), in_=w[g][:, a:b], func=ACT.Copy, scale=lift[:, g : g + 1])
+
+        def round_on_vector(g, a, b):
+            nc.vector.tensor_scalar(out=pairs_part(g, a, b), in0=w[g][:, a:b], scalar1=lift[:, g : g + 1], scalar2=None, op0=ALU.mult)
+
+        def turn(g, u):
+            nc.tensor.transpose(turned[g][:, u, :], pairs[g][u][:].bitcast(F32), ident[:])
+
+        round_on_scalar(0, 0, HALF)
+        round_on_scalar(0, HALF, PAGE)
+        round_on_scalar(1, 0, HALF)
+        round_on_vector(1, HALF, PAGE)
+        for a, b in zip(last_cuts, last_cuts[1:]):
+            round_on_vector(last, a, b)
         w_bf = []
         for g in range(PAGES):
-            pairs = sb.tile([P, 2, P, 2], BF16, name=f"pairs{g}", align_bytes=64)
-            if g == 0:
-                nc.scalar.activation(out=pairs[:], in_=dealt[g], func=ACT.Copy, scale=lift[:, g : g + 1])
-            else:
-                nc.vector.tensor_scalar(out=pairs[:], in0=dealt[g], scalar1=lift[:, g : g + 1], scalar2=None, op0=ALU.mult)
-            pair_words = pairs[:].rearrange("q u s e -> q (u s e)").bitcast(F32)
-            turned = ps.tile([P, 2, NQ], F32, name=f"turned{g}", tag=f"turn{g}")
             for u in range(2):
-                nc.tensor.transpose(turned[:, u, :], pair_words[:, u * P : (u + 1) * P], ident[:])
+                turn(g, u)
             wb = sb.tile([P, NQ * PACK], BF16, name=f"w_bf{g}", align_bytes=64)
-            nc.scalar.copy(out=wb[:].bitcast(F32).rearrange("s (q u) -> s q u", u=2), in_=turned[:].rearrange("s u q -> s q u"))
+            nc.scalar.copy(out=wb[:].bitcast(F32).rearrange("s (q u) -> s q u", u=2), in_=turned[g][:].rearrange("s u q -> s q u"))
             w_bf.append(wb)
 
-        total = sb.tile([P, 1], F32, name="total")
-        inv = sb.tile([P, 1], F32, name="inv")
-        lifted = sb.tile([P, PAGES], F32, name="lifted", tag="p2", align_bytes=64)
-        nc.vector.scalar_tensor_tensor(out=lifted[:], in0=sums[:], scalar=1.0, in1=lift[:], op0=ALU.mult, op1=ALU.mult, accum_out=total[:])
-        v_codes = sb.tile([P, PAGES * DV], U32, name="v_codes", tag="w1", align_bytes=64)
+        v_codes = laid.tile([P, PAGES * DV], U32, name="v_codes", align_bytes=64, offset=P_LAST_AT)
         nc.vector.tensor_copy(v_codes[:], v_pool[:].bitcast(U32).indirect(v_list[:]))
-        nc.vector.reciprocal(inv[:], total[:])
 
-        half = DV // 2
-        acc = [ps.tile([P, half], F32, name=f"acc{h}", tag=("acc", "turn3")[h]) for h in range(2)]
+        cols_half = DV // 2
+        acc = [ps.tile([P, cols_half], F32, name=f"acc{h}", tag=("acc", "turn3")[h]) for h in range(2)]
         for g in range(PAGES):
             w_codes = sb.tile([P, NQ], U32, name=f"w_codes{g}", align_bytes=64)
-            w_bytes = sb.tile([P, NQ], U8, name=f"w_bytes{g}", align_bytes=64)
-            nc.vector.quantize_mx(out=w_codes[:].bitcast(FP8X4), scales=w_bytes[:], in_=w_bf[g][:])
+            w_plane = sb.tile([P, NQ], U8, name=f"w_plane{g}", align_bytes=64)
+            nc.vector.quantize_mx(out=w_codes[:].bitcast(FP8X4), scales=w_plane[:], in_=w_bf[g][:])
             for h in range(2):
-                cols = slice(g * DV + h * half, g * DV + (h + 1) * half)
+                cols = slice(g * DV + h * cols_half, g * DV + (h + 1) * cols_half)
                 nc.tensor.matmul_mx(
-                    out=acc[h][:], lhsT=w_codes[:].bitcast(FP8X4), lhsT_scale=w_bytes[:],
-                    rhs=v_codes[:, cols].bitcast(FP8X4), rhs_scale=v_bytes[:, cols],
-                    start=(g == 0), stop=(g == PAGES - 1),
+                    out=acc[h][:], lhsT=w_codes[:].bitcast(FP8X4), lhsT_scale=w_plane[:],
+                    rhs=v_codes[:, cols].bitcast(FP8X4), rhs_scale=v_plane[:, cols],
+                    start=(g == 0), stop=(g == last),
                 )
 
-        y0 = sb.tile([P, half], F32, name="y0")
-        y1 = sb.tile([P, half], F32, name="y1")
+        total = sb.tile([P, PAGES + 1], F32, name="total")
+        nc.scalar.activation(out=total[:, 0:1], in_=sums[:, 0:1], func=ACT.Copy, scale=lift[:, 0:1])
+        for j in range(1, PAGES + 1):
+            g = min(j, last)
+            nc.scalar.activation(out=total[:, j : j + 1], in_=sums[:, j : j + 1], func=ACT.Identity, scale=lift[:, g : g + 1], bias=total[:, j - 1 : j])
+        inv = sb.tile([P, 1], F32, name="inv")
+        nc.vector.reciprocal(inv[:], total[:, PAGES:])
+
+        y0 = sb.tile([P, cols_half], F32, name="y0")
+        y1 = sb.tile([P, cols_half], F32, name="y1")
         nc.scalar.activation(out=y0[:], in_=acc[0][:], func=ACT.Copy, scale=inv[:])
         nc.vector.tensor_scalar(out=y1[:], in0=acc[1][:], scalar1=inv[:], scalar2=None, op0=ALU.mult)
-        nc.scalar.dma_start(out=out[0, :, :half], in_=y0[:])
-        nc.sync.dma_start(out=out[0, :, half:], in_=y1[:])
+        nc.scalar.dma_start(out=out[0, :, :cols_half], in_=y0[:])
+        nc.sync.dma_start(out=out[0, :, cols_half:], in_=y1[:])

@@ -52,11 +52,15 @@ def tile_attend_pkv8_qpk_kernel(tc, q_words, q_scales, k_words, k_scales, v_word
         ones = sb.tile([P, P], F32, name="ones", align_bytes=64)
         ident = sb.tile([P, P], F32, name="ident", align_bytes=64)
 
+        def load_q_plane(queue, r):
+            queue.dma_start(out=q_plane[r:P:32, :].bitcast(I32), in_=q_scales[0, 0, r:16:4, :].bitcast(I32))
+
         k_dram = k_words[0].rearrange("p t r -> p (t r)").bitcast(I32)
         nc.sync.dma_start(out=k_scale_pool[K_ROW:, :].bitcast(I32), in_=k_scales[0].bitcast(I32))
         nc.sync.dma_start(k_list[:], offs)
         nc.sync.dma_start(out=k_pool[:, : T // 2], in_=k_dram[:, : T // 2])
         nc.sync.dma_start(v_list[:], voffs)
+        load_q_plane(nc.sync, 3)
         nc.sync.dma_start(out=k_pool[:, T // 2 :], in_=k_dram[:, T // 2 :])
         nc.sync.dma_start(out=q_codes[:], in_=q_words[0, 0].rearrange("p q r -> p (q r)").bitcast(I32))
         nc.scalar.dma_start(out=vs_cols[:], in_=vs[0].rearrange("(p c) -> p c", p=P))
@@ -64,8 +68,8 @@ def tile_attend_pkv8_qpk_kernel(tc, q_words, q_scales, k_words, k_scales, v_word
             out=v_scale_pool[V_ROW:64, :].bitcast(I32).rearrange("p (u e) -> p u e", u=POOL_PAGES),
             in_=v_scales.rearrange("u f e -> f u e").bitcast(I32),
         )
-        for r in range(4):
-            nc.scalar.dma_start(out=q_plane[r:P:32, :].bitcast(I32), in_=q_scales[0, 0, r:16:4, :].bitcast(I32))
+        for r in range(3):
+            load_q_plane(nc.scalar, r)
 
         nc.vector.memset(k_scale_pool[:K_ROW, :].bitcast(I32), 0)
         nc.vector.memset(v_scale_pool[:V_ROW, :].bitcast(I32), 0)

@@ -144,11 +144,10 @@ def tile_attend_pkv8_qpk_kernel(tc, q_words, q_scales, k_words, k_scales, v_word
         exp_part(last, EXP_HEAD, P, PAGES)
         weigh(0, WEIGH_HEAD, PAGE)
         weigh(1, 0, PAGE)
-        last_cuts = (0, HALF, HALF + P, PAGE)
-        for a, b in zip(last_cuts, last_cuts[1:]):
-            weigh(last, a, b)
+        weigh(last, 0, PAGE - P)
+        weigh(last, PAGE - P, PAGE)
 
-        pairs = [[sb.tile([P, HALF], BF16, name=f"pairs{g}_{u}", align_bytes=64) for u in range(2)] for g in range(PAGES)]
+        pairs = [[sb.tile([P, HALF], BF16, name=f"pairs{g}_{u}", tag=f"pairs{g}_{u}", align_bytes=64) for u in range(2)] for g in range(PAGES)]
         turned = [ps.tile([P, 2, NQ], F32, name=f"turned{g}", tag=f"turn{g}") for g in range(PAGES)]
 
         def pairs_part(g, a, b):
@@ -168,6 +167,7 @@ def tile_attend_pkv8_qpk_kernel(tc, q_words, q_scales, k_words, k_scales, v_word
         round_on_scalar(0, HALF, PAGE)
         round_on_scalar(1, 0, HALF)
         round_on_vector(1, HALF, PAGE)
+        last_cuts = (0, HALF, PAGE - P, PAGE)
         for a, b in zip(last_cuts, last_cuts[1:]):
             round_on_vector(last, a, b)
         w_bf = []
@@ -178,12 +178,18 @@ def tile_attend_pkv8_qpk_kernel(tc, q_words, q_scales, k_words, k_scales, v_word
             nc.scalar.copy(out=wb[:].bitcast(F32).rearrange("s (q u) -> s q u", u=2), in_=turned[g][:].rearrange("s u q -> s q u"))
             w_bf.append(wb)
 
-        v_codes = laid.tile([P, PAGES * DV], U32, name="v_codes", align_bytes=64, offset=P_LAST_AT)
-        nc.vector.tensor_copy(v_codes[:], v_pool[:].bitcast(U32).indirect(v_list[:]))
+        first_cols = last * DV // LIST_ROWS
+        v_first = laid.tile([P, last * DV], U32, name="v_first", align_bytes=64, offset=P_LAST_AT)
+        nc.vector.tensor_copy(v_first[:], v_pool[:].bitcast(U32).indirect(v_list[:, :first_cols]))
+        v_codes = [v_first[:, g * DV : (g + 1) * DV] for g in range(last)]
 
         cols_half = DV // 2
         acc = [ps.tile([P, cols_half], F32, name=f"acc{h}", tag=("acc", "turn3")[h]) for h in range(2)]
         for g in range(PAGES):
+            if g == last:
+                v_last = sb.tile([P, DV], U32, name="v_last", tag=f"pairs{last}_1", align_bytes=64)
+                nc.vector.tensor_copy(v_last[:], v_pool[:].bitcast(U32).indirect(v_list[:, first_cols:]))
+                v_codes.append(v_last[:])
             w_codes = sb.tile([P, NQ], U32, name=f"w_codes{g}", align_bytes=64)
             w_plane = sb.tile([P, NQ], U8, name=f"w_plane{g}", align_bytes=64)
             nc.vector.quantize_mx(out=w_codes[:].bitcast(FP8X4), scales=w_plane[:], in_=w_bf[g][:])
@@ -191,7 +197,7 @@ def tile_attend_pkv8_qpk_kernel(tc, q_words, q_scales, k_words, k_scales, v_word
                 cols = slice(g * DV + h * cols_half, g * DV + (h + 1) * cols_half)
                 nc.tensor.matmul_mx(
                     out=acc[h][:], lhsT=w_codes[:].bitcast(FP8X4), lhsT_scale=w_plane[:],
-                    rhs=v_codes[:, cols].bitcast(FP8X4), rhs_scale=v_plane[:, cols],
+                    rhs=v_codes[g][:, h * cols_half : (h + 1) * cols_half].bitcast(FP8X4), rhs_scale=v_plane[:, cols],
                     start=(g == 0), stop=(g == last),
                 )
 

@@ -118,7 +118,8 @@ def tile_attend_pkv8_qpk_kernel(tc, q_words, q_scales, k_words, k_scales, v_word
 
         last = PAGES - 1
         neg_page = sb.tile([P, PAGES], F32, name="neg_page")
-        sums = sb.tile([P, PAGES + 1], F32, name="sums")
+        sums = sb.tile([P, PAGES, 2], F32, name="sums")
+        nc.vector.memset(sums[:], 0.0)
         p = [sb.tile([P, PAGE], F32, name=f"p{g}", align_bytes=64) for g in range(last)]
         p.append(laid.tile([P, PAGE], F32, name="p_last", align_bytes=64, offset=P_LAST_AT))
         w = [sb.tile([P, PAGE], F32, name=f"w{g}", align_bytes=64) for g in range(PAGES)]
@@ -126,7 +127,7 @@ def tile_attend_pkv8_qpk_kernel(tc, q_words, q_scales, k_words, k_scales, v_word
         def exp_part(g, a, b, col):
             nc.scalar.activation(
                 out=p[g][:].rearrange("q (u s e) -> q u s e", u=2, e=2)[:, :, a:b], in_=scores[g].rearrange("q (s u e) -> q u s e", u=2, e=2)[:, :, a:b],
-                func=ACT.Exp, bias=neg_page[:, g : g + 1], scale=1.0, accum_out=sums[:, col : col + 1],
+                func=ACT.Exp, bias=neg_page[:, g : g + 1], scale=1.0, accum_out=sums[:, g, col : col + 1],
             )
 
         def weigh(g, a, b):
@@ -134,14 +135,14 @@ def tile_attend_pkv8_qpk_kernel(tc, q_words, q_scales, k_words, k_scales, v_word
 
         for g in range(PAGES):
             nc.vector.tensor_reduce(out=neg_page[:, g : g + 1], in_=scores[g], axis=ALONG_FREE, op=ALU.max, negate=True)
-            exp_part(g, 0, P if g < last else EXP_HEAD, g)
+            exp_part(g, 0, P if g < last else EXP_HEAD, 0)
 
         weigh(0, 0, WEIGH_HEAD)
         neg_max = sb.tile([P, 1], F32, name="neg_max")
         nc.vector.tensor_reduce(out=neg_max[:], in_=neg_page[:], axis=ALONG_FREE, op=ALU.min)
         lift = sb.tile([P, PAGES], F32, name="lift")
         nc.scalar.activation(out=lift[:], in_=neg_page[:], func=ACT.Exp, bias=neg_max[:], scale=-1.0)
-        exp_part(last, EXP_HEAD, P, PAGES)
+        exp_part(last, EXP_HEAD, P, 1)
         weigh(0, WEIGH_HEAD, PAGE)
         weigh(1, 0, PAGE)
         weigh(last, 0, PAGE - P)
@@ -174,7 +175,7 @@ def tile_attend_pkv8_qpk_kernel(tc, q_words, q_scales, k_words, k_scales, v_word
         for g in range(PAGES):
             for u in range(2):
                 turn(g, u)
-            wb = sb.tile([P, NQ * PACK], BF16, name=f"w_bf{g}", align_bytes=64)
+            wb = sb.tile([P, NQ * PACK], BF16, name=f"w_bf{g}", tag=f"w_bf{g}", align_bytes=64)
             nc.scalar.copy(out=wb[:].bitcast(F32).rearrange("s (q u) -> s q u", u=2), in_=turned[g][:].rearrange("s u q -> s q u"))
             w_bf.append(wb)
 
@@ -201,13 +202,11 @@ def tile_attend_pkv8_qpk_kernel(tc, q_words, q_scales, k_words, k_scales, v_word
                     start=(g == 0), stop=(g == last),
                 )
 
-        total = sb.tile([P, PAGES + 1], F32, name="total")
-        nc.scalar.activation(out=total[:, 0:1], in_=sums[:, 0:1], func=ACT.Copy, scale=lift[:, 0:1])
-        for j in range(1, PAGES + 1):
-            g = min(j, last)
-            nc.scalar.activation(out=total[:, j : j + 1], in_=sums[:, j : j + 1], func=ACT.Identity, scale=lift[:, g : g + 1], bias=total[:, j - 1 : j])
-        inv = sb.tile([P, 1], F32, name="inv")
-        nc.vector.reciprocal(inv[:], total[:, PAGES:])
+        total = sb.tile([P, 1], F32, name="total")
+        lifted = sb.tile([P, PAGES, 2], F32, name="lifted", tag=f"pairs{last}_0", align_bytes=64)
+        nc.vector.scalar_tensor_tensor(out=lifted[:], in0=sums[:], scalar=1.0, in1=lift[:].unsqueeze(2).to_broadcast([P, PAGES, 2]), op0=ALU.mult, op1=ALU.mult, accum_out=total[:])
+        inv = sb.tile([P, 1], F32, name="inv", tag=f"w_bf{last}", align_bytes=64)
+        nc.vector.reciprocal(inv[:], total[:])
 
         y0 = sb.tile([P, cols_half], F32, name="y0")
         y1 = sb.tile([P, cols_half], F32, name="y1")

@@ -23,11 +23,19 @@ PAGES = 3
 POOL_PAGES = 8
 PACK = 4
 LIST_ROWS = 16
-K_ROW = 112
-V_ROW = 48
+ROW0 = 32
+ROW_STEP = 4
 EXP_HEAD = 96
 WEIGH_HEAD = 320
 P_LAST_AT = POOL_PAGES * DV * 4
+K_POOL_AT = P_LAST_AT + PAGE * 4
+K_POOL_END = K_POOL_AT + T * 4
+Q_CODES_AT = K_POOL_END + NQ
+K_ROWS_AT = Q_CODES_AT + NQ * 4
+V_ROWS_AT = K_ROWS_AT + PAGES * PAGE
+EARLY_WORDS = (V_ROWS_AT + NQ - (K_POOL_END - NQ)) // 4
+K_HEAD = 512
+K_MID = 2048
 FLOPS = 301989888
 
 
@@ -40,42 +48,46 @@ def tile_attend_pkv8_qpk_kernel(tc, q_words, q_scales, k_words, k_scales, v_word
 
         k_list = sb.tile([P, PAGES * PAGE // LIST_ROWS], U16, name="k_list")
         v_list = sb.tile([P, PAGES * DV // LIST_ROWS], U16, name="v_list")
-        k_pool = sb.tile([P, T], I32, name="k_pool", align_bytes=64)
+        k_pool = laid.tile([P, T], I32, name="k_pool", align_bytes=64, offset=K_POOL_AT)
+        k_head = sb.tile([P, K_HEAD], I32, name="k_head", align_bytes=64)
         k_scale_pool = sb.tile([P, T], U8, name="k_scale_pool", align_bytes=64)
         v_scale_pool = laid.tile([P, POOL_PAGES * DV], U8, name="v_scale_pool", align_bytes=64, offset=0)
         vs_pool = sb.tile([P, T], F32, name="vs_pool", align_bytes=64)
         vs_cols = sb.tile([P, T // P], F32, name="vs_cols", align_bytes=64)
-        q_codes = sb.tile([P, NQ], I32, name="q_codes", align_bytes=64)
-        q_plane = sb.tile([P, NQ], U8, name="q_plane", align_bytes=64)
+        q_codes = laid.tile([P, NQ], I32, name="q_codes", align_bytes=64, offset=Q_CODES_AT)
+        q_plane = laid.tile([P, NQ], U8, name="q_plane", align_bytes=64, offset=K_POOL_END)
         k_plane = sb.tile([P, PAGES * PAGE], U8, name="k_plane", align_bytes=64)
         v_plane = sb.tile([P, PAGES * DV], U8, name="v_plane", align_bytes=64)
-        ones = sb.tile([P, P], F32, name="ones", align_bytes=64)
+        early = laid.tile([P, EARLY_WORDS], I32, name="early", align_bytes=64, offset=K_POOL_END - NQ)
+        ramp = early[:, :P]
         ident = sb.tile([P, P], F32, name="ident", align_bytes=64)
 
         def load_q_plane(queue, r):
             queue.dma_start(out=q_plane[r:P:32, :].bitcast(I32), in_=q_scales[0, 0, r:16:4, :].bitcast(I32))
 
         k_dram = k_words[0].rearrange("p t r -> p (t r)").bitcast(I32)
-        nc.sync.dma_start(out=k_scale_pool[K_ROW:, :].bitcast(I32), in_=k_scales[0].bitcast(I32))
+        rows = slice(ROW0, ROW0 + 16 * ROW_STEP, ROW_STEP)
+        nc.gpsimd.iota(ramp, pattern=[[1, P]], base=0, channel_multiplier=-1)
+        nc.vector.memset(k_scale_pool[:].bitcast(I32), 0)
+        nc.vector.memset(v_scale_pool[:].bitcast(I32), 0)
+        nc.vector.tensor_scalar(out=ident[:], in0=ramp, scalar1=0.0, scalar2=None, op0=ALU.is_equal)
+        nc.sync.dma_start(out=k_head[:], in_=k_dram[:, :K_HEAD])
         nc.sync.dma_start(k_list[:], offs)
-        nc.sync.dma_start(out=k_pool[:, : T // 2], in_=k_dram[:, : T // 2])
         nc.sync.dma_start(v_list[:], voffs)
-        load_q_plane(nc.sync, 3)
-        nc.sync.dma_start(out=k_pool[:, T // 2 :], in_=k_dram[:, T // 2 :])
-        nc.sync.dma_start(out=q_codes[:], in_=q_words[0, 0].rearrange("p q r -> p (q r)").bitcast(I32))
-        nc.scalar.dma_start(out=vs_cols[:], in_=vs[0].rearrange("(p c) -> p c", p=P))
-        nc.scalar.dma_start(
-            out=v_scale_pool[V_ROW:64, :].bitcast(I32).rearrange("p (u e) -> p u e", u=POOL_PAGES),
+        nc.sync.dma_start(out=k_scale_pool[rows, :].bitcast(I32), in_=k_scales[0].bitcast(I32))
+        nc.sync.dma_start(
+            out=v_scale_pool[rows, :].bitcast(I32).rearrange("p (u e) -> p u e", u=POOL_PAGES),
             in_=v_scales.rearrange("u f e -> f u e").bitcast(I32),
         )
-        for r in range(3):
-            load_q_plane(nc.scalar, r)
-
-        nc.vector.memset(k_scale_pool[:K_ROW, :].bitcast(I32), 0)
-        nc.vector.memset(v_scale_pool[:V_ROW, :].bitcast(I32), 0)
-        nc.vector.memset(v_scale_pool[64:, :].bitcast(I32), 0)
-        nc.gpsimd.memset(ones[:], 1.0)
-        nc.gpsimd.affine_select(out=ident[:], in_=ones[:], pattern=[[-1, P]], compare_op=ALU.is_equal, fill=0.0, base=0, channel_multiplier=1)
+        nc.sync.dma_start(out=k_pool[:, K_HEAD:K_MID], in_=k_dram[:, K_HEAD:K_MID])
+        for r in range(2):
+            load_q_plane(nc.sync, r)
+        nc.sync.dma_start(out=k_pool[:, K_MID:], in_=k_dram[:, K_MID:])
+        nc.sync.dma_start(out=q_codes[:], in_=q_words[0, 0].rearrange("p q r -> p (q r)").bitcast(I32))
+        for r in range(2, 4):
+            load_q_plane(nc.sync, r)
+        nc.scalar.dma_start(out=vs_cols[:], in_=vs[0].rearrange("(p c) -> p c", p=P))
+        nc.vector.tensor_copy(k_pool[:, :K_HEAD], k_head[:])
 
         vs_view = vs_pool[:].rearrange("p (page u i j c) -> p u j page i c", page=POOL_PAGES, u=2, i=16, c=PACK)
         for j in range(4):
@@ -86,12 +98,12 @@ def tile_attend_pkv8_qpk_kernel(tc, q_words, q_scales, k_words, k_scales, v_word
                     nc.tensor.transpose(spread[:, c, :], vs_cols[:, col : col + 1].to_broadcast([P, P]), ident[:])
                 nc.scalar.activation(out=vs_view[:, u, j], in_=spread[:].rearrange("p c (page i) -> p page i c", i=16), func=ACT.Copy)
 
-        k_rows = sb.tile([P, PAGES * PAGE], U8, name="k_rows", align_bytes=64)
+        k_rows = laid.tile([P, PAGES * PAGE], U8, name="k_rows", align_bytes=64, offset=K_ROWS_AT)
         nc.vector.tensor_copy(k_rows[:], k_scale_pool[:].indirect(k_list[:]))
         for r in range(4):
-            nc.sync.dma_start(out=k_plane[r:P:32, :].bitcast(I32), in_=k_rows[K_ROW + r : P : 4, :].bitcast(I32))
+            nc.sync.dma_start(out=k_plane[r:P:32, :].bitcast(I32), in_=k_rows[ROW0 + ROW_STEP * r : ROW0 + 16 * ROW_STEP : 4 * ROW_STEP, :].bitcast(I32))
 
-        v_rows = sb.tile([P, PAGES * DV], U8, name="v_rows", align_bytes=64)
+        v_rows = laid.tile([P, PAGES * DV], U8, name="v_rows", align_bytes=64, offset=V_ROWS_AT)
         nc.vector.tensor_copy(v_rows[:], v_scale_pool[:].indirect(v_list[:]))
         v_pool = laid.tile([P, POOL_PAGES * DV], I32, name="v_pool", align_bytes=64, offset=0)
         nc.sync.dma_start(
@@ -99,7 +111,7 @@ def tile_attend_pkv8_qpk_kernel(tc, q_words, q_scales, k_words, k_scales, v_word
             in_=v_words.rearrange("u p e r -> p u (e r)").bitcast(I32),
         )
         for r in range(4):
-            nc.sync.dma_start(out=v_plane[r:P:32, :].bitcast(I32), in_=v_rows[V_ROW + r : 64 : 4, :].bitcast(I32))
+            nc.sync.dma_start(out=v_plane[r:P:32, :].bitcast(I32), in_=v_rows[ROW0 + ROW_STEP * r : ROW0 + 16 * ROW_STEP : 4 * ROW_STEP, :].bitcast(I32))
 
         def k_offsets(g, a, b):
             return k_list[:, (g * PAGE + a) // LIST_ROWS : (g * PAGE + b) // LIST_ROWS]

@@ -27,14 +27,15 @@ ROW0 = 32
 ROW_STEP = 4
 EXP_HEAD = 96
 WEIGH_HEAD = 320
-P_LAST_AT = POOL_PAGES * DV * 4
+P_LAST_AT = 0
 K_POOL_AT = P_LAST_AT + PAGE * 4
 K_POOL_END = K_POOL_AT + T * 4
 Q_CODES_AT = K_POOL_END + NQ
 K_ROWS_AT = Q_CODES_AT + NQ * 4
 V_ROWS_AT = K_ROWS_AT + PAGES * PAGE
-EARLY_WORDS = (V_ROWS_AT + NQ - (K_POOL_END - NQ)) // 4
-K_HEAD = 512
+V_SCALE_AT = V_ROWS_AT + PAGES * DV
+EARLY_WORDS = (V_SCALE_AT + NQ - (K_POOL_END - NQ)) // 4
+K_HEAD = 384
 K_MID = 2048
 FLOPS = 301989888
 
@@ -51,7 +52,7 @@ def tile_attend_pkv8_qpk_kernel(tc, q_words, q_scales, k_words, k_scales, v_word
         k_pool = laid.tile([P, T], I32, name="k_pool", align_bytes=64, offset=K_POOL_AT)
         k_head = sb.tile([P, K_HEAD], I32, name="k_head", align_bytes=64)
         k_scale_pool = sb.tile([P, T], U8, name="k_scale_pool", align_bytes=64)
-        v_scale_pool = laid.tile([P, POOL_PAGES * DV], U8, name="v_scale_pool", align_bytes=64, offset=0)
+        v_scale_pool = laid.tile([P, POOL_PAGES * DV], U8, name="v_scale_pool", align_bytes=64, offset=V_SCALE_AT)
         vs_pool = sb.tile([P, T], F32, name="vs_pool", align_bytes=64)
         vs_cols = sb.tile([P, T // P], F32, name="vs_cols", align_bytes=64)
         q_codes = laid.tile([P, NQ], I32, name="q_codes", align_bytes=64, offset=Q_CODES_AT)
@@ -69,19 +70,19 @@ def tile_attend_pkv8_qpk_kernel(tc, q_words, q_scales, k_words, k_scales, v_word
         rows = slice(ROW0, ROW0 + 16 * ROW_STEP, ROW_STEP)
         nc.gpsimd.iota(ramp, pattern=[[1, P]], base=0, channel_multiplier=-1)
         nc.vector.memset(k_scale_pool[:].bitcast(I32), 0)
-        nc.vector.memset(v_scale_pool[:].bitcast(I32), 0)
         nc.vector.tensor_scalar(out=ident[:], in0=ramp, scalar1=0.0, scalar2=None, op0=ALU.is_equal)
+        nc.vector.memset(v_scale_pool[:].bitcast(I32), 0)
         nc.sync.dma_start(out=k_head[:], in_=k_dram[:, :K_HEAD])
         nc.sync.dma_start(k_list[:], offs)
         nc.sync.dma_start(v_list[:], voffs)
         nc.sync.dma_start(out=k_scale_pool[rows, :].bitcast(I32), in_=k_scales[0].bitcast(I32))
+        nc.sync.dma_start(out=k_pool[:, K_HEAD:K_MID], in_=k_dram[:, K_HEAD:K_MID])
+        for r in range(2):
+            load_q_plane(nc.sync, r)
         nc.sync.dma_start(
             out=v_scale_pool[rows, :].bitcast(I32).rearrange("p (u e) -> p u e", u=POOL_PAGES),
             in_=v_scales.rearrange("u f e -> f u e").bitcast(I32),
         )
-        nc.sync.dma_start(out=k_pool[:, K_HEAD:K_MID], in_=k_dram[:, K_HEAD:K_MID])
-        for r in range(2):
-            load_q_plane(nc.sync, r)
         nc.sync.dma_start(out=k_pool[:, K_MID:], in_=k_dram[:, K_MID:])
         nc.sync.dma_start(out=q_codes[:], in_=q_words[0, 0].rearrange("p q r -> p (q r)").bitcast(I32))
         for r in range(2, 4):
@@ -105,7 +106,7 @@ def tile_attend_pkv8_qpk_kernel(tc, q_words, q_scales, k_words, k_scales, v_word
 
         v_rows = laid.tile([P, PAGES * DV], U8, name="v_rows", align_bytes=64, offset=V_ROWS_AT)
         nc.vector.tensor_copy(v_rows[:], v_scale_pool[:].indirect(v_list[:]))
-        v_pool = laid.tile([P, POOL_PAGES * DV], I32, name="v_pool", align_bytes=64, offset=0)
+        v_pool = laid.tile([P, POOL_PAGES * DV], I32, name="v_pool", align_bytes=64, offset=V_SCALE_AT)
         nc.sync.dma_start(
             out=v_pool[:].rearrange("p (u e) -> p u e", u=POOL_PAGES),
             in_=v_words.rearrange("u p e r -> p u (e r)").bitcast(I32),

@@ -25,8 +25,6 @@ PACK = 4
 LIST_ROWS = 16
 ROW0 = 32
 ROW_STEP = 4
-EXP_HEAD = 96
-WEIGH_HEAD = 320
 P_LAST_AT = 0
 K_POOL_AT = P_LAST_AT + PAGE * 4
 K_POOL_END = K_POOL_AT + T * 4
@@ -117,6 +115,10 @@ def tile_attend_pkv8_qpk_kernel(tc, q_words, q_scales, k_words, k_scales, v_word
         def k_offsets(g, a, b):
             return k_list[:, (g * PAGE + a) // LIST_ROWS : (g * PAGE + b) // LIST_ROWS]
 
+        vs_first = PAGE + HALF
+        vs_late = sb.tile([P, PAGES * PAGE - vs_first], F32, name="vs_late", align_bytes=64)
+        nc.scalar.activation(out=vs_late[:], in_=vs_pool[:].indirect(k_list[:, vs_first // LIST_ROWS :]), func=ACT.Copy)
+
         scores = []
         for g in range(PAGES):
             k_codes = sb.tile([P, PAGE], U32, name=f"k_codes{g}", align_bytes=64)
@@ -130,67 +132,68 @@ def tile_attend_pkv8_qpk_kernel(tc, q_words, q_scales, k_words, k_scales, v_word
             scores.append(bank[:])
 
         last = PAGES - 1
-        neg_page = sb.tile([P, PAGES], F32, name="neg_page")
-        sums = sb.tile([P, PAGES, 2], F32, name="sums")
-        nc.vector.memset(sums[:], 0.0)
+        neg = sb.tile([P, PAGES + 1], F32, name="neg")
+        neg_max = neg[:, PAGES:]
+        sums = sb.tile([P, PAGES + 1], F32, name="sums")
+        lift = sb.tile([P, PAGES + 1], F32, name="lift")
         p = [sb.tile([P, PAGE], F32, name=f"p{g}", align_bytes=64) for g in range(last)]
-        p.append(laid.tile([P, PAGE], F32, name="p_last", align_bytes=64, offset=P_LAST_AT))
-        w = [sb.tile([P, PAGE], F32, name=f"w{g}", align_bytes=64) for g in range(PAGES)]
+        p_last = [
+            laid.tile([P, HALF], F32, name="p_last0", align_bytes=64, offset=P_LAST_AT),
+            sb.tile([P, HALF], F32, name="p_last1", align_bytes=64),
+        ]
+        pairs = [[sb.tile([P, HALF], BF16, name=f"pairs{g}_{u}", tag=f"pairs{g}_{u}", align_bytes=64) for u in range(2)] for g in range(PAGES)]
 
-        def exp_part(g, a, b, col):
+        def dealt(g):
+            return scores[g].rearrange("q (s u e) -> q u s e", u=2, e=2)
+
+        def exp_last(u, col):
             nc.scalar.activation(
-                out=p[g][:].rearrange("q (u s e) -> q u s e", u=2, e=2)[:, :, a:b], in_=scores[g].rearrange("q (s u e) -> q u s e", u=2, e=2)[:, :, a:b],
-                func=ACT.Exp, bias=neg_page[:, g : g + 1], scale=1.0, accum_out=sums[:, g, col : col + 1],
+                out=p_last[u][:].rearrange("q (s e) -> q s e", e=2), in_=dealt(last)[:, u],
+                func=ACT.Exp, bias=neg[:, col : col + 1], scale=1.0, accum_out=sums[:, col : col + 1],
             )
 
-        def weigh(g, a, b):
-            nc.vector.tensor_tensor(w[g][:, a:b], vs_pool[:].indirect(k_offsets(g, a, b)), p[g][:, a:b], ALU.mult)
+        def weigh(g, u):
+            w = sb.tile([P, HALF], F32, name=f"w{g}_{u}", align_bytes=64)
+            nc.vector.tensor_tensor(w[:], vs_pool[:].indirect(k_offsets(g, u * HALF, (u + 1) * HALF)), p[g][:, u * HALF : (u + 1) * HALF], ALU.mult)
+            return w
+
+        def weigh_and_round(g, u, p_half, col):
+            at = g * PAGE + u * HALF - vs_first
+            nc.vector.scalar_tensor_tensor(
+                out=pairs[g][u][:], in0=p_half, scalar=lift[:, col : col + 1], in1=vs_late[:, at : at + HALF], op0=ALU.mult, op1=ALU.mult
+            )
 
         for g in range(PAGES):
-            nc.vector.tensor_reduce(out=neg_page[:, g : g + 1], in_=scores[g], axis=ALONG_FREE, op=ALU.max, negate=True)
-            exp_part(g, 0, P if g < last else EXP_HEAD, 0)
+            nc.vector.tensor_reduce(out=neg[:, g : g + 1], in_=scores[g], axis=ALONG_FREE, op=ALU.max, negate=True)
+            if g < last:
+                nc.scalar.activation(
+                    out=p[g][:].rearrange("q (u s e) -> q u s e", u=2, e=2), in_=dealt(g),
+                    func=ACT.Exp, bias=neg[:, g : g + 1], scale=1.0, accum_out=sums[:, g : g + 1],
+                )
+        exp_last(0, last)
 
-        weigh(0, 0, WEIGH_HEAD)
-        neg_max = sb.tile([P, 1], F32, name="neg_max")
-        nc.vector.tensor_reduce(out=neg_max[:], in_=neg_page[:], axis=ALONG_FREE, op=ALU.min)
-        lift = sb.tile([P, PAGES], F32, name="lift")
-        nc.scalar.activation(out=lift[:], in_=neg_page[:], func=ACT.Exp, bias=neg_max[:], scale=-1.0)
-        exp_part(last, EXP_HEAD, P, 1)
-        weigh(0, WEIGH_HEAD, PAGE)
-        weigh(1, 0, PAGE)
-        weigh(last, 0, PAGE - P)
-        weigh(last, PAGE - P, PAGE)
+        w00 = weigh(0, 0)
+        nc.vector.tensor_reduce(out=neg_max, in_=neg[:, :PAGES], axis=ALONG_FREE, op=ALU.min)
+        nc.scalar.activation(out=lift[:], in_=neg[:], func=ACT.Exp, bias=neg_max, scale=-1.0)
+        exp_last(1, PAGES)
+        w01 = weigh(0, 1)
+        w10 = weigh(1, 0)
 
-        pairs = [[sb.tile([P, HALF], BF16, name=f"pairs{g}_{u}", tag=f"pairs{g}_{u}", align_bytes=64) for u in range(2)] for g in range(PAGES)]
-        turned = [ps.tile([P, 2, NQ], F32, name=f"turned{g}", tag=f"turn{g}") for g in range(PAGES)]
+        nc.vector.tensor_scalar(out=pairs[1][0][:], in0=w10[:], scalar1=lift[:, 1:2], scalar2=None, op0=ALU.mult)
+        weigh_and_round(1, 1, p[1][:, HALF:], 1)
+        for u, w in enumerate((w00, w01)):
+            nc.scalar.activation(out=pairs[0][u][:], in_=w[:], func=ACT.Copy, scale=lift[:, 0:1])
+        weigh_and_round(last, 0, p_last[0][:], last)
+        weigh_and_round(last, 1, p_last[1][:], PAGES)
 
-        def pairs_part(g, a, b):
-            u = a // HALF
-            return pairs[g][u][:, a - u * HALF : b - u * HALF]
-
-        def round_on_scalar(g, a, b):
-            nc.scalar.activation(out=pairs_part(g, a, b), in_=w[g][:, a:b], func=ACT.Copy, scale=lift[:, g : g + 1])
-
-        def round_on_vector(g, a, b):
-            nc.vector.tensor_scalar(out=pairs_part(g, a, b), in0=w[g][:, a:b], scalar1=lift[:, g : g + 1], scalar2=None, op0=ALU.mult)
-
-        def turn(g, u):
-            nc.tensor.transpose(turned[g][:, u, :], pairs[g][u][:].bitcast(F32), ident[:])
-
-        round_on_scalar(0, 0, HALF)
-        round_on_scalar(0, HALF, PAGE)
-        round_on_scalar(1, 0, HALF)
-        round_on_vector(1, HALF, PAGE)
-        last_cuts = (0, HALF, PAGE - P, PAGE)
-        for a, b in zip(last_cuts, last_cuts[1:]):
-            round_on_vector(last, a, b)
-        w_bf = []
-        for g in range(PAGES):
+        order = (1, 0, last)
+        w_bf = {}
+        for g in order:
+            turned = ps.tile([P, 2, NQ], F32, name=f"turned{g}", tag=f"turn{g}")
             for u in range(2):
-                turn(g, u)
-            wb = sb.tile([P, NQ * PACK], BF16, name=f"w_bf{g}", tag=f"w_bf{g}", align_bytes=64)
-            nc.scalar.copy(out=wb[:].bitcast(F32).rearrange("s (q u) -> s q u", u=2), in_=turned[g][:].rearrange("s u q -> s q u"))
-            w_bf.append(wb)
+                nc.tensor.transpose(turned[:, u, :], pairs[g][u][:].bitcast(F32), ident[:])
+            w_bf[g] = sb.tile([P, NQ * PACK], BF16, name=f"w_bf{g}", tag=f"w_bf{g}", align_bytes=64)
+            nc.scalar.copy(out=w_bf[g][:].bitcast(F32).rearrange("s (q u) -> s q u", u=2), in_=turned[:].rearrange("s u q -> s q u"))
 
         first_cols = last * DV // LIST_ROWS
         v_first = laid.tile([P, last * DV], U32, name="v_first", align_bytes=64, offset=P_LAST_AT)
@@ -199,7 +202,7 @@ def tile_attend_pkv8_qpk_kernel(tc, q_words, q_scales, k_words, k_scales, v_word
 
         cols_half = DV // 2
         acc = [ps.tile([P, cols_half], F32, name=f"acc{h}", tag=("acc", "turn3")[h]) for h in range(2)]
-        for g in range(PAGES):
+        for g in order:
             if g == last:
                 v_last = sb.tile([P, DV], U32, name="v_last", tag=f"pairs{last}_1", align_bytes=64)
                 nc.vector.tensor_copy(v_last[:], v_pool[:].bitcast(U32).indirect(v_list[:, first_cols:]))
@@ -212,12 +215,12 @@ def tile_attend_pkv8_qpk_kernel(tc, q_words, q_scales, k_words, k_scales, v_word
                 nc.tensor.matmul_mx(
                     out=acc[h][:], lhsT=w_codes[:].bitcast(FP8X4), lhsT_scale=w_plane[:],
                     rhs=v_codes[g][:, h * cols_half : (h + 1) * cols_half].bitcast(FP8X4), rhs_scale=v_plane[:, cols],
-                    start=(g == 0), stop=(g == last),
+                    start=(g == order[0]), stop=(g == last),
                 )
 
         total = sb.tile([P, 1], F32, name="total")
-        lifted = sb.tile([P, PAGES, 2], F32, name="lifted", tag=f"pairs{last}_0", align_bytes=64)
-        nc.vector.scalar_tensor_tensor(out=lifted[:], in0=sums[:], scalar=1.0, in1=lift[:].unsqueeze(2).to_broadcast([P, PAGES, 2]), op0=ALU.mult, op1=ALU.mult, accum_out=total[:])
+        lifted = sb.tile([P, PAGES + 1], F32, name="lifted", tag=f"pairs{last}_0", align_bytes=64)
+        nc.vector.scalar_tensor_tensor(out=lifted[:], in0=sums[:], scalar=1.0, in1=lift[:], op0=ALU.mult, op1=ALU.mult, accum_out=total[:])
         inv = sb.tile([P, 1], F32, name="inv", tag=f"w_bf{last}", align_bytes=64)
         nc.vector.reciprocal(inv[:], total[:])
 

@@ -121,14 +121,15 @@ def tile_attend_pkv8_qpk_kernel(tc, q_words, q_scales, k_words, k_scales, v_word
 
         scores = []
         for g in range(PAGES):
-            k_codes = sb.tile([P, PAGE], U32, name=f"k_codes{g}", align_bytes=64)
-            nc.vector.tensor_copy(k_codes[:], k_pool[:].bitcast(U32).indirect(k_offsets(g, 0, PAGE)))
             bank = ps.tile([P, PAGE], F32, name=f"score{g}")
-            nc.tensor.matmul_mx(
-                out=bank[:], lhsT=q_codes[:].bitcast(FP8X4), lhsT_scale=q_plane[:],
-                rhs=k_codes[:].bitcast(FP8X4), rhs_scale=k_plane[:, g * PAGE : (g + 1) * PAGE],
-                start=True, stop=True,
-            )
+            for a in (0, HALF):
+                k_codes = sb.tile([P, HALF], U32, name=f"k_codes{g}_{a}", align_bytes=64)
+                nc.vector.tensor_copy(k_codes[:], k_pool[:].bitcast(U32).indirect(k_offsets(g, a, a + HALF)))
+                nc.tensor.matmul_mx(
+                    out=bank[:, a : a + HALF], lhsT=q_codes[:].bitcast(FP8X4), lhsT_scale=q_plane[:],
+                    rhs=k_codes[:].bitcast(FP8X4), rhs_scale=k_plane[:, g * PAGE + a : g * PAGE + a + HALF],
+                    start=True, stop=True,
+                )
             scores.append(bank[:])
 
         last = PAGES - 1

@@ -121,78 +121,95 @@ def tile_attend_pkv8_qpk_kernel(tc, q_words, q_scales, k_words, k_scales, v_word
 
         scores = []
         for g in range(PAGES):
-            bank = ps.tile([P, PAGE], F32, name=f"score{g}")
+            if g == 0:
+                halves = [ps.tile([P, HALF], F32, name=f"score0_{h}", tag=("acc", "score0")[h])[:] for h in range(2)]
+                first_halves = halves
+            else:
+                bank = ps.tile([P, PAGE], F32, name=f"score{g}")
+                halves = [bank[:, :HALF], bank[:, HALF:]]
             for a in (0, HALF):
                 k_codes = sb.tile([P, HALF], U32, name=f"k_codes{g}_{a}", align_bytes=64)
                 nc.vector.tensor_copy(k_codes[:], k_pool[:].bitcast(U32).indirect(k_offsets(g, a, a + HALF)))
                 nc.tensor.matmul_mx(
-                    out=bank[:, a : a + HALF], lhsT=q_codes[:].bitcast(FP8X4), lhsT_scale=q_plane[:],
+                    out=halves[a // HALF], lhsT=q_codes[:].bitcast(FP8X4), lhsT_scale=q_plane[:],
                     rhs=k_codes[:].bitcast(FP8X4), rhs_scale=k_plane[:, g * PAGE + a : g * PAGE + a + HALF],
                     start=True, stop=True,
                 )
-            scores.append(bank[:])
+            scores.append(None if g == 0 else bank[:])
 
         last = PAGES - 1
-        neg = sb.tile([P, PAGES + 1], F32, name="neg")
-        neg_max = neg[:, PAGES:]
-        sums = sb.tile([P, PAGES + 1], F32, name="sums")
-        lift = sb.tile([P, PAGES + 1], F32, name="lift")
+        parts = PAGES + 1
+        neg = sb.tile([P, parts + 1], F32, name="neg")
+        neg_max = neg[:, parts:]
+        sums = sb.tile([P, parts + 1], F32, name="sums")
+        lift = sb.tile([P, parts + 1], F32, name="lift")
         p = [sb.tile([P, PAGE], F32, name=f"p{g}", align_bytes=64) for g in range(last)]
         p_last = [
             laid.tile([P, HALF], F32, name="p_last0", align_bytes=64, offset=P_LAST_AT),
             sb.tile([P, HALF], F32, name="p_last1", align_bytes=64),
         ]
-        pairs = [[sb.tile([P, HALF], BF16, name=f"pairs{g}_{u}", tag=f"pairs{g}_{u}", align_bytes=64) for u in range(2)] for g in range(PAGES)]
+        pairs_first = sb.tile([P, PAGE], BF16, name="pairs_first", align_bytes=64)
+        pairs = [[pairs_first[:, :HALF], pairs_first[:, HALF:]]]
+        for g in range(1, PAGES):
+            pairs.append([sb.tile([P, HALF], BF16, name=f"pairs{g}_{u}", tag=f"pairs{g}_{u}", align_bytes=64)[:] for u in range(2)])
 
         def dealt(g):
             return scores[g].rearrange("q (s u e) -> q u s e", u=2, e=2)
 
-        def exp_last(u, col):
+        def exp_half(g, u, p_half, col):
             nc.scalar.activation(
-                out=p_last[u][:].rearrange("q (s e) -> q s e", e=2), in_=dealt(last)[:, u],
+                out=p_half.rearrange("q (s e) -> q s e", e=2), in_=dealt(g)[:, u],
                 func=ACT.Exp, bias=neg[:, col : col + 1], scale=1.0, accum_out=sums[:, col : col + 1],
             )
 
-        def weigh(g, u):
-            w = sb.tile([P, HALF], F32, name=f"w{g}_{u}", align_bytes=64)
-            nc.vector.tensor_tensor(w[:], vs_pool[:].indirect(k_offsets(g, u * HALF, (u + 1) * HALF)), p[g][:, u * HALF : (u + 1) * HALF], ALU.mult)
-            return w
+        def weigh(g, u, w):
+            nc.vector.tensor_tensor(w, vs_pool[:].indirect(k_offsets(g, u * HALF, (u + 1) * HALF)), p[g][:, u * HALF : (u + 1) * HALF], ALU.mult)
 
         def weigh_and_round(g, u, p_half, col):
             at = g * PAGE + u * HALF - vs_first
             nc.vector.scalar_tensor_tensor(
-                out=pairs[g][u][:], in0=p_half, scalar=lift[:, col : col + 1], in1=vs_late[:, at : at + HALF], op0=ALU.mult, op1=ALU.mult
+                out=pairs[g][u], in0=p_half, scalar=lift[:, col : col + 1], in1=vs_late[:, at : at + HALF], op0=ALU.mult, op1=ALU.mult
             )
 
-        for g in range(PAGES):
-            nc.vector.tensor_reduce(out=neg[:, g : g + 1], in_=scores[g], axis=ALONG_FREE, op=ALU.max, negate=True)
-            if g < last:
-                nc.scalar.activation(
-                    out=p[g][:].rearrange("q (u s e) -> q u s e", u=2, e=2), in_=dealt(g),
-                    func=ACT.Exp, bias=neg[:, g : g + 1], scale=1.0, accum_out=sums[:, g : g + 1],
-                )
-        exp_last(0, last)
+        def words_of_half(tile, h):
+            return tile[:].rearrange("q (u h s e) -> q h u s e", u=2, h=2, e=2)[:, h]
 
-        w00 = weigh(0, 0)
-        nc.vector.tensor_reduce(out=neg_max, in_=neg[:, :PAGES], axis=ALONG_FREE, op=ALU.min)
+        for h in range(2):
+            nc.vector.tensor_reduce(out=neg[:, h : h + 1], in_=first_halves[h], axis=ALONG_FREE, op=ALU.max, negate=True)
+            nc.scalar.activation(
+                out=words_of_half(p[0], h), in_=first_halves[h].rearrange("q (s u e) -> q u s e", u=2, e=2),
+                func=ACT.Exp, bias=neg[:, h : h + 1], scale=1.0, accum_out=sums[:, h : h + 1],
+            )
+        nc.vector.tensor_reduce(out=neg[:, 2:3], in_=scores[1], axis=ALONG_FREE, op=ALU.max, negate=True)
+        nc.scalar.activation(
+            out=p[1][:].rearrange("q (u s e) -> q u s e", u=2, e=2), in_=dealt(1),
+            func=ACT.Exp, bias=neg[:, 2:3], scale=1.0, accum_out=sums[:, 2:3],
+        )
+        nc.vector.tensor_reduce(out=neg[:, 3:4], in_=scores[last], axis=ALONG_FREE, op=ALU.max, negate=True)
+        exp_half(last, 0, p_last[0][:], 3)
+
+        w0 = sb.tile([P, PAGE], F32, name="w0", align_bytes=64)
+        w10 = sb.tile([P, HALF], F32, name="w10", align_bytes=64)
+        weigh(0, 0, w0[:, :HALF])
+        nc.vector.tensor_reduce(out=neg_max, in_=neg[:, :parts], axis=ALONG_FREE, op=ALU.min)
         nc.scalar.activation(out=lift[:], in_=neg[:], func=ACT.Exp, bias=neg_max, scale=-1.0)
-        exp_last(1, PAGES)
-        w01 = weigh(0, 1)
-        w10 = weigh(1, 0)
+        exp_half(last, 1, p_last[1][:], parts)
+        weigh(0, 1, w0[:, HALF:])
+        weigh(1, 0, w10[:])
 
-        nc.vector.tensor_scalar(out=pairs[1][0][:], in0=w10[:], scalar1=lift[:, 1:2], scalar2=None, op0=ALU.mult)
-        weigh_and_round(1, 1, p[1][:, HALF:], 1)
-        for u, w in enumerate((w00, w01)):
-            nc.scalar.activation(out=pairs[0][u][:], in_=w[:], func=ACT.Copy, scale=lift[:, 0:1])
-        weigh_and_round(last, 0, p_last[0][:], last)
-        weigh_and_round(last, 1, p_last[1][:], PAGES)
+        nc.vector.tensor_scalar(out=pairs[1][0], in0=w10[:], scalar1=lift[:, 2:3], scalar2=None, op0=ALU.mult)
+        weigh_and_round(1, 1, p[1][:, HALF:], 2)
+        for h in range(2):
+            nc.scalar.activation(out=words_of_half(pairs_first, h), in_=words_of_half(w0, h), func=ACT.Copy, scale=lift[:, h : h + 1])
+        weigh_and_round(last, 0, p_last[0][:], 3)
+        weigh_and_round(last, 1, p_last[1][:], parts)
 
         order = (1, 0, last)
         w_bf = {}
         for g in order:
             turned = ps.tile([P, 2, NQ], F32, name=f"turned{g}", tag=f"turn{g}")
             for u in range(2):
-                nc.tensor.transpose(turned[:, u, :], pairs[g][u][:].bitcast(F32), ident[:])
+                nc.tensor.transpose(turned[:, u, :], pairs[g][u].bitcast(F32), ident[:])
             w_bf[g] = sb.tile([P, NQ * PACK], BF16, name=f"w_bf{g}", tag=f"w_bf{g}", align_bytes=64)
             nc.scalar.copy(out=w_bf[g][:].bitcast(F32).rearrange("s (q u) -> s q u", u=2), in_=turned[:].rearrange("s u q -> s q u"))
 
@@ -220,7 +237,7 @@ def tile_attend_pkv8_qpk_kernel(tc, q_words, q_scales, k_words, k_scales, v_word
                 )
 
         total = sb.tile([P, 1], F32, name="total")
-        lifted = sb.tile([P, PAGES + 1], F32, name="lifted", tag=f"pairs{last}_0", align_bytes=64)
+        lifted = sb.tile([P, parts + 1], F32, name="lifted", tag=f"pairs{last}_0", align_bytes=64)
         nc.vector.scalar_tensor_tensor(out=lifted[:], in0=sums[:], scalar=1.0, in1=lift[:], op0=ALU.mult, op1=ALU.mult, accum_out=total[:])
         inv = sb.tile([P, 1], F32, name="inv", tag=f"w_bf{last}", align_bytes=64)
         nc.vector.reciprocal(inv[:], total[:])

@@ -115,9 +115,9 @@ def tile_attend_pkv8_qpk_kernel(tc, q_words, q_scales, k_words, k_scales, v_word
         def k_offsets(g, a, b):
             return k_list[:, (g * PAGE + a) // LIST_ROWS : (g * PAGE + b) // LIST_ROWS]
 
-        vs_first = PAGE + HALF
+        vs_first = 0
         vs_late = sb.tile([P, PAGES * PAGE - vs_first], F32, name="vs_late", align_bytes=64)
-        nc.scalar.activation(out=vs_late[:], in_=vs_pool[:].indirect(k_list[:, vs_first // LIST_ROWS :]), func=ACT.Copy)
+        nc.scalar.activation(out=vs_late[:], in_=vs_pool[:].indirect(k_list[:]), func=ACT.Copy)
 
         scores = []
         for g in range(PAGES):
@@ -163,7 +163,7 @@ def tile_attend_pkv8_qpk_kernel(tc, q_words, q_scales, k_words, k_scales, v_word
             )
 
         def weigh(g, u, w):
-            nc.vector.tensor_tensor(w, vs_pool[:].indirect(k_offsets(g, u * HALF, (u + 1) * HALF)), p[g][:, u * HALF : (u + 1) * HALF], ALU.mult)
+            nc.vector.tensor_tensor(w, vs_late[:, g * PAGE + u * HALF : g * PAGE + (u + 1) * HALF], p[g][:, u * HALF : (u + 1) * HALF], ALU.mult)
 
         def weigh_and_round(g, u, p_half, col):
             at = g * PAGE + u * HALF - vs_first

@@ -204,6 +204,9 @@ def tile_attend_pkv8_qpk_kernel(tc, q_words, q_scales, k_words, k_scales, v_word
         weigh_and_round(last, 0, p_last[0][:], 3)
         weigh_and_round(last, 1, p_last[1][:], parts)
 
+        def query_cuts(g):
+            return ((0, NQ // 2), (NQ // 2, NQ)) if g == last else ((0, NQ),)
+
         order = (1, 0, last)
         w_bf = {}
         for g in order:
@@ -211,23 +214,20 @@ def tile_attend_pkv8_qpk_kernel(tc, q_words, q_scales, k_words, k_scales, v_word
             for u in range(2):
                 nc.tensor.transpose(turned[:, u, :], pairs[g][u].bitcast(F32), ident[:])
             w_bf[g] = sb.tile([P, NQ * PACK], BF16, name=f"w_bf{g}", tag=f"w_bf{g}", align_bytes=64)
-            nc.scalar.copy(out=w_bf[g][:].bitcast(F32).rearrange("s (q u) -> s q u", u=2), in_=turned[:].rearrange("s u q -> s q u"))
+            for a, b in query_cuts(g):
+                nc.scalar.copy(out=w_bf[g][:, PACK * a : PACK * b].bitcast(F32).rearrange("s (q u) -> s q u", u=2), in_=turned[:, :, a:b].rearrange("s u q -> s q u"))
 
-        first_cols = last * DV // LIST_ROWS
-        v_first = laid.tile([P, last * DV], U32, name="v_first", align_bytes=64, offset=P_LAST_AT)
-        nc.vector.tensor_copy(v_first[:], v_pool[:].bitcast(U32).indirect(v_list[:, :first_cols]))
-        v_codes = [v_first[:, g * DV : (g + 1) * DV] for g in range(last)]
+        v_all = laid.tile([P, PAGES * DV], U32, name="v_all", align_bytes=64, offset=P_LAST_AT)
+        nc.vector.tensor_copy(v_all[:], v_pool[:].bitcast(U32).indirect(v_list[:]))
+        v_codes = [v_all[:, g * DV : (g + 1) * DV] for g in range(PAGES)]
 
         cols_half = DV // 2
         acc = [ps.tile([P, cols_half], F32, name=f"acc{h}", tag=("acc", "turn3")[h]) for h in range(2)]
         for g in order:
-            if g == last:
-                v_last = sb.tile([P, DV], U32, name="v_last", tag=f"pairs{last}_1", align_bytes=64)
-                nc.vector.tensor_copy(v_last[:], v_pool[:].bitcast(U32).indirect(v_list[:, first_cols:]))
-                v_codes.append(v_last[:])
             w_codes = sb.tile([P, NQ], U32, name=f"w_codes{g}", align_bytes=64)
             w_plane = sb.tile([P, NQ], U8, name=f"w_plane{g}", align_bytes=64)
-            nc.vector.quantize_mx(out=w_codes[:].bitcast(FP8X4), scales=w_plane[:], in_=w_bf[g][:])
+            for a, b in query_cuts(g):
+                nc.vector.quantize_mx(out=w_codes[:, a:b].bitcast(FP8X4), scales=w_plane[:, a:b], in_=w_bf[g][:, PACK * a : PACK * b])
             for h in range(2):
                 cols = slice(g * DV + h * cols_half, g * DV + (h + 1) * cols_half)
                 nc.tensor.matmul_mx(
@@ -237,7 +237,7 @@ def tile_attend_pkv8_qpk_kernel(tc, q_words, q_scales, k_words, k_scales, v_word
                 )
 
         total = sb.tile([P, 1], F32, name="total")
-        lifted = sb.tile([P, parts + 1], F32, name="lifted", tag=f"pairs{last}_0", align_bytes=64)
+        lifted = sb.tile([P, parts + 1], F32, name="lifted", tag=f"pairs{last}_1", align_bytes=64)
         nc.vector.scalar_tensor_tensor(out=lifted[:], in0=sums[:], scalar=1.0, in1=lift[:], op0=ALU.mult, op1=ALU.mult, accum_out=total[:])
         inv = sb.tile([P, 1], F32, name="inv", tag=f"w_bf{last}", align_bytes=64)
         nc.vector.reciprocal(inv[:], total[:])

@@ -33,7 +33,7 @@ K_ROWS_AT = Q_CODES_AT + NQ * 4
 V_ROWS_AT = K_ROWS_AT + PAGES * PAGE
 V_SCALE_AT = V_ROWS_AT + PAGES * DV
 EARLY_WORDS = (V_SCALE_AT + NQ - (K_POOL_END - NQ)) // 4
-K_HEAD = 384
+K_HEAD = 512
 K_MID = 2048
 FLOPS = 301989888
 
@@ -88,14 +88,13 @@ def tile_attend_pkv8_qpk_kernel(tc, q_words, q_scales, k_words, k_scales, v_word
         nc.scalar.dma_start(out=vs_cols[:], in_=vs[0].rearrange("(p c) -> p c", p=P))
         nc.vector.tensor_copy(k_pool[:, :K_HEAD], k_head[:])
 
-        vs_view = vs_pool[:].rearrange("p (page u i j c) -> p u j page i c", page=POOL_PAGES, u=2, i=16, c=PACK)
-        for j in range(4):
-            for u in range(2):
-                spread = ps.tile([P, PACK, P], F32, name=f"spread{j}_{u}", tag=f"turn{(2 * j + u) % 4}")
-                for c in range(PACK):
-                    col = 8 * j + 4 * (c // 2) + 2 * u + c % 2
-                    nc.tensor.transpose(spread[:, c, :], vs_cols[:, col : col + 1].to_broadcast([P, P]), ident[:])
-                nc.scalar.activation(out=vs_view[:, u, j], in_=spread[:].rearrange("p c (page i) -> p page i c", i=16), func=ACT.Copy)
+        vs_view = vs_pool[:].rearrange("p (n j c) -> p j n c", n=P, c=PACK)
+        for j in range(T // P // PACK):
+            spread = ps.tile([P, PACK, P], F32, name=f"spread{j}", tag=f"turn{j % 4}")
+            for c in range(PACK):
+                col = PACK * j + c
+                nc.tensor.transpose(spread[:, c, :], vs_cols[:, col : col + 1].to_broadcast([P, P]), ident[:])
+            nc.scalar.activation(out=vs_view[:, j], in_=spread[:].rearrange("p c n -> p n c"), func=ACT.Copy)
 
         k_rows = laid.tile([P, PAGES * PAGE], U8, name="k_rows", align_bytes=64, offset=K_ROWS_AT)
         nc.vector.tensor_copy(k_rows[:], k_scale_pool[:].indirect(k_list[:]))
@@ -115,9 +114,9 @@ def tile_attend_pkv8_qpk_kernel(tc, q_words, q_scales, k_words, k_scales, v_word
         def k_offsets(g, a, b):
             return k_list[:, (g * PAGE + a) // LIST_ROWS : (g * PAGE + b) // LIST_ROWS]
 
-        vs_first = 0
-        vs_late = sb.tile([P, PAGES * PAGE - vs_first], F32, name="vs_late", align_bytes=64)
-        nc.scalar.activation(out=vs_late[:], in_=vs_pool[:].indirect(k_list[:]), func=ACT.Copy)
+        vs_listed = sb.tile([P, PAGES * PAGE], F32, name="vs_listed", align_bytes=64)
+        nc.scalar.activation(out=vs_listed[:], in_=vs_pool[:].indirect(k_list[:]), func=ACT.Copy)
+        vs_dealt = vs_listed[:].rearrange("q (g s u e) -> q g u s e", g=PAGES, u=2, e=2)
 
         scores = []
         for g in range(PAGES):
@@ -156,19 +155,21 @@ def tile_attend_pkv8_qpk_kernel(tc, q_words, q_scales, k_words, k_scales, v_word
         def dealt(g):
             return scores[g].rearrange("q (s u e) -> q u s e", u=2, e=2)
 
+        def in_pairs(half):
+            return half.rearrange("q (s e) -> q s e", e=2)
+
         def exp_half(g, u, p_half, col):
             nc.scalar.activation(
-                out=p_half.rearrange("q (s e) -> q s e", e=2), in_=dealt(g)[:, u],
+                out=in_pairs(p_half), in_=dealt(g)[:, u],
                 func=ACT.Exp, bias=neg[:, col : col + 1], scale=1.0, accum_out=sums[:, col : col + 1],
             )
 
         def weigh(g, u, w):
-            nc.vector.tensor_tensor(w, vs_late[:, g * PAGE + u * HALF : g * PAGE + (u + 1) * HALF], p[g][:, u * HALF : (u + 1) * HALF], ALU.mult)
+            nc.vector.tensor_tensor(in_pairs(w), in_pairs(p[g][:, u * HALF : (u + 1) * HALF]), vs_dealt[:, g, u], ALU.mult)
 
         def weigh_and_round(g, u, p_half, col):
-            at = g * PAGE + u * HALF - vs_first
             nc.vector.scalar_tensor_tensor(
-                out=pairs[g][u], in0=p_half, scalar=lift[:, col : col + 1], in1=vs_late[:, at : at + HALF], op0=ALU.mult, op1=ALU.mult
+                out=in_pairs(pairs[g][u]), in0=in_pairs(p_half), scalar=lift[:, col : col + 1], in1=vs_dealt[:, g, u], op0=ALU.mult, op1=ALU.mult
             )
 
         def words_of_half(tile, h):

@@ -33,7 +33,7 @@ K_ROWS_AT = Q_CODES_AT + NQ * 4
 V_ROWS_AT = K_ROWS_AT + PAGES * PAGE
 V_SCALE_AT = V_ROWS_AT + PAGES * DV
 EARLY_WORDS = (V_SCALE_AT + NQ - (K_POOL_END - NQ)) // 4
-K_HEAD = 512
+K_HEAD = 640
 K_MID = 2048
 FLOPS = 301989888
 

@@ -126,12 +126,14 @@ def tile_attend_pkv8_qpk_kernel(tc, q_words, q_scales, k_words, k_scales, v_word
             else:
                 bank = ps.tile([P, PAGE], F32, name=f"score{g}")
                 halves = [bank[:, :HALF], bank[:, HALF:]]
+            width = PAGE if g == 0 else HALF
             for a in (0, HALF):
-                k_codes = sb.tile([P, HALF], U32, name=f"k_codes{g}_{a}", align_bytes=64)
-                nc.vector.tensor_copy(k_codes[:], k_pool[:].bitcast(U32).indirect(k_offsets(g, a, a + HALF)))
+                if a % width == 0:
+                    k_codes = sb.tile([P, width], U32, name=f"k_codes{g}_{a}", align_bytes=64)
+                    nc.vector.tensor_copy(k_codes[:], k_pool[:].bitcast(U32).indirect(k_offsets(g, a, a + width)))
                 nc.tensor.matmul_mx(
                     out=halves[a // HALF], lhsT=q_codes[:].bitcast(FP8X4), lhsT_scale=q_plane[:],
-                    rhs=k_codes[:].bitcast(FP8X4), rhs_scale=k_plane[:, g * PAGE + a : g * PAGE + a + HALF],
+                    rhs=k_codes[:, a % width : a % width + HALF].bitcast(FP8X4), rhs_scale=k_plane[:, g * PAGE + a : g * PAGE + a + HALF],
                     start=True, stop=True,
                 )
             scores.append(None if g == 0 else bank[:])

from contextlib import ExitStack

import concourse.mybir as mybir

F32 = mybir.dt.float32
BF16 = mybir.dt.bfloat16
I32 = mybir.dt.int32
U32 = mybir.dt.uint32
U16 = mybir.dt.uint16
U8 = mybir.dt.uint8
FP8X4 = mybir.dt.float8_e4m3fn_x4
ALU = mybir.AluOpType
ACT = mybir.ActivationFunctionType
ALONG_FREE = mybir.AxisListType.X

P = 128
T = 4096
NQ = 128
DV = 256
PAGE = 512
HALF = PAGE // 2
PAGES = 3
POOL_PAGES = 8
PACK = 4
LIST_ROWS = 16
ROW0 = 32
ROW_STEP = 4
P_LAST_AT = 0
K_POOL_AT = P_LAST_AT + PAGE * 4
K_POOL_END = K_POOL_AT + T * 4
Q_CODES_AT = K_POOL_END + NQ
K_ROWS_AT = Q_CODES_AT + NQ * 4
V_ROWS_AT = K_ROWS_AT + PAGES * PAGE
V_SCALE_AT = V_ROWS_AT + PAGES * DV
EARLY_WORDS = (V_SCALE_AT + NQ - (K_POOL_END - NQ)) // 4
K_HEAD = 640
K_MID = 2048
FLOPS = 301989888


def tile_attend_pkv8_qpk_kernel(tc, q_words, q_scales, k_words, k_scales, v_words, v_scales, vs, offs, voffs, out):
    nc = tc.nc
    with ExitStack() as ctx:
        sb = ctx.enter_context(tc.tile_pool(name="sb", bufs=1))
        laid = ctx.enter_context(tc.tile_pool(name="laid", bufs=1))
        ps = ctx.enter_context(tc.psum_pool(name="ps", bufs=1))

        k_list = sb.tile([P, PAGES * PAGE // LIST_ROWS], U16, name="k_list")
        v_list = sb.tile([P, PAGES * DV // LIST_ROWS], U16, name="v_list")
        k_pool = laid.tile([P, T], I32, name="k_pool", align_bytes=64, offset=K_POOL_AT)
        k_head = sb.tile([P, K_HEAD], I32, name="k_head", align_bytes=64)
        k_scale_pool = sb.tile([P, T], U8, name="k_scale_pool", align_bytes=64)
        v_scale_pool = laid.tile([P, POOL_PAGES * DV], U8, name="v_scale_pool", align_bytes=64, offset=V_SCALE_AT)
        vs_pool = sb.tile([P, T], F32, name="vs_pool", align_bytes=64)
        vs_cols = sb.tile([P, T // P], F32, name="vs_cols", align_bytes=64)
        q_codes = laid.tile([P, NQ], I32, name="q_codes", align_bytes=64, offset=Q_CODES_AT)
        q_plane = laid.tile([P, NQ], U8, name="q_plane", align_bytes=64, offset=K_POOL_END)
        k_plane = sb.tile([P, PAGES * PAGE], U8, name="k_plane", align_bytes=64)
        v_plane = sb.tile([P, PAGES * DV], U8, name="v_plane", align_bytes=64)
        early = laid.tile([P, EARLY_WORDS], I32, name="early", align_bytes=64, offset=K_POOL_END - NQ)
        ramp = early[:, :P]
        ident = sb.tile([P, P], F32, name="ident", align_bytes=64)

        def load_q_plane(queue, r):
            queue.dma_start(out=q_plane[r:P:32, :].bitcast(I32), in_=q_scales[0, 0, r:16:4, :].bitcast(I32))

        k_dram = k_words[0].rearrange("p t r -> p (t r)").bitcast(I32)
        rows = slice(ROW0, ROW0 + 16 * ROW_STEP, ROW_STEP)
        nc.gpsimd.iota(ramp, pattern=[[1, P]], base=0, channel_multiplier=-1)
        nc.vector.memset(k_scale_pool[:].bitcast(I32), 0)
        nc.vector.tensor_scalar(out=ident[:], in0=ramp, scalar1=0.0, scalar2=None, op0=ALU.is_equal)
        nc.vector.memset(v_scale_pool[:].bitcast(I32), 0)
        nc.sync.dma_start(out=k_head[:], in_=k_dram[:, :K_HEAD])
        nc.sync.dma_start(k_list[:], offs)
        nc.sync.dma_start(v_list[:], voffs)
        nc.sync.dma_start(out=k_scale_pool[rows, :].bitcast(I32), in_=k_scales[0].bitcast(I32))
        nc.sync.dma_start(out=k_pool[:, K_HEAD:K_MID], in_=k_dram[:, K_HEAD:K_MID])
        for r in range(2):
            load_q_plane(nc.sync, r)
        nc.sync.dma_start(
            out=v_scale_pool[rows, :].bitcast(I32).rearrange("p (u e) -> p u e", u=POOL_PAGES),
            in_=v_scales.rearrange("u f e -> f u e").bitcast(I32),
        )
        nc.sync.dma_start(out=k_pool[:, K_MID:], in_=k_dram[:, K_MID:])
        nc.sync.dma_start(out=q_codes[:], in_=q_words[0, 0].rearrange("p q r -> p (q r)").bitcast(I32))
        for r in range(2, 4):
            load_q_plane(nc.sync, r)
        nc.scalar.dma_start(out=vs_cols[:], in_=vs[0].rearrange("(p c) -> p c", p=P))
        nc.vector.tensor_copy(k_pool[:, :K_HEAD], k_head[:])

        vs_view = vs_pool[:].rearrange("p (n j c) -> p j n c", n=P, c=PACK)
        for j in range(T // P // PACK):
            spread = ps.tile([P, PACK, P], F32, name=f"spread{j}", tag=f"turn{j % 4}")
            for c in range(PACK):
                col = PACK * j + c
                nc.tensor.transpose(spread[:, c, :], vs_cols[:, col : col + 1].to_broadcast([P, P]), ident[:])
            nc.scalar.activation(out=vs_view[:, j], in_=spread[:].rearrange("p c n -> p n c"), func=ACT.Copy)

        k_rows = laid.tile([P, PAGES * PAGE], U8, name="k_rows", align_bytes=64, offset=K_ROWS_AT)
        nc.vector.tensor_copy(k_rows[:], k_scale_pool[:].indirect(k_list[:]))
        for r in range(4):
            nc.sync.dma_start(out=k_plane[r:P:32, :].bitcast(I32), in_=k_rows[ROW0 + ROW_STEP * r : ROW0 + 16 * ROW_STEP : 4 * ROW_STEP, :].bitcast(I32))

        v_rows = laid.tile([P, PAGES * DV], U8, name="v_rows", align_bytes=64, offset=V_ROWS_AT)
        nc.vector.tensor_copy(v_rows[:], v_scale_pool[:].indirect(v_list[:]))
        v_pool = laid.tile([P, POOL_PAGES * DV], I32, name="v_pool", align_bytes=64, offset=V_SCALE_AT)
        nc.sync.dma_start(
            out=v_pool[:].rearrange("p (u e) -> p u e", u=POOL_PAGES),
            in_=v_words.rearrange("u p e r -> p u (e r)").bitcast(I32),
        )
        for r in range(4):
            nc.sync.dma_start(out=v_plane[r:P:32, :].bitcast(I32), in_=v_rows[ROW0 + ROW_STEP * r : ROW0 + 16 * ROW_STEP : 4 * ROW_STEP, :].bitcast(I32))

        def k_offsets(g, a, b):
            return k_list[:, (g * PAGE + a) // LIST_ROWS : (g * PAGE + b) // LIST_ROWS]

        vs_listed = sb.tile([P, PAGES * PAGE], F32, name="vs_listed", align_bytes=64)
        nc.scalar.activation(out=vs_listed[:], in_=vs_pool[:].indirect(k_list[:]), func=ACT.Copy)
        vs_dealt = vs_listed[:].rearrange("q (g s u e) -> q g u s e", g=PAGES, u=2, e=2)

        scores = []
        for g in range(PAGES):
            if g == 0:
                halves = [ps.tile([P, HALF], F32, name=f"score0_{h}", tag=("acc", "score0")[h])[:] for h in range(2)]
                first_halves = halves
            else:
                bank = ps.tile([P, PAGE], F32, name=f"score{g}")
                halves = [bank[:, :HALF], bank[:, HALF:]]
            width = PAGE if g == 0 else HALF
            for a in (0, HALF):
                if a % width == 0:
                    k_codes = sb.tile([P, width], U32, name=f"k_codes{g}_{a}", align_bytes=64)
                    nc.vector.tensor_copy(k_codes[:], k_pool[:].bitcast(U32).indirect(k_offsets(g, a, a + width)))
                nc.tensor.matmul_mx(
                    out=halves[a // HALF], lhsT=q_codes[:].bitcast(FP8X4), lhsT_scale=q_plane[:],
                    rhs=k_codes[:, a % width : a % width + HALF].bitcast(FP8X4), rhs_scale=k_plane[:, g * PAGE + a : g * PAGE + a + HALF],
                    start=True, stop=True,
                )
            scores.append(None if g == 0 else bank[:])

        last = PAGES - 1
        parts = PAGES + 1
        neg = sb.tile([P, parts + 1], F32, name="neg")
        neg_max = neg[:, parts:]
        sums = sb.tile([P, parts + 1], F32, name="sums")
        lift = sb.tile([P, parts + 1], F32, name="lift")
        p = [sb.tile([P, PAGE], F32, name=f"p{g}", align_bytes=64) for g in range(last)]
        p_last = [
            laid.tile([P, HALF], F32, name="p_last0", align_bytes=64, offset=P_LAST_AT),
            sb.tile([P, HALF], F32, name="p_last1", align_bytes=64),
        ]
        pairs_first = sb.tile([P, PAGE], BF16, name="pairs_first", align_bytes=64)
        pairs = [[pairs_first[:, :HALF], pairs_first[:, HALF:]]]
        for g in range(1, PAGES):
            pairs.append([sb.tile([P, HALF], BF16, name=f"pairs{g}_{u}", tag=f"pairs{g}_{u}", align_bytes=64)[:] for u in range(2)])

        def dealt(g):
            return scores[g].rearrange("q (s u e) -> q u s e", u=2, e=2)

        def in_pairs(half):
            return half.rearrange("q (s e) -> q s e", e=2)

        def exp_half(g, u, p_half, col):
            nc.scalar.activation(
                out=in_pairs(p_half), in_=dealt(g)[:, u],
                func=ACT.Exp, bias=neg[:, col : col + 1], scale=1.0, accum_out=sums[:, col : col + 1],
            )

        def weigh(g, u, w):
            nc.vector.tensor_tensor(in_pairs(w), in_pairs(p[g][:, u * HALF : (u + 1) * HALF]), vs_dealt[:, g, u], ALU.mult)

        def weigh_and_round(g, u, p_half, col):
            nc.vector.scalar_tensor_tensor(
                out=in_pairs(pairs[g][u]), in0=in_pairs(p_half), scalar=lift[:, col : col + 1], in1=vs_dealt[:, g, u], op0=ALU.mult, op1=ALU.mult
            )

        def words_of_half(tile, h):
            return tile[:].rearrange("q (u h s e) -> q h u s e", u=2, h=2, e=2)[:, h]

        for h in range(2):
            nc.vector.tensor_reduce(out=neg[:, h : h + 1], in_=first_halves[h], axis=ALONG_FREE, op=ALU.max, negate=True)
            nc.scalar.activation(
                out=words_of_half(p[0], h), in_=first_halves[h].rearrange("q (s u e) -> q u s e", u=2, e=2),
                func=ACT.Exp, bias=neg[:, h : h + 1], scale=1.0, accum_out=sums[:, h : h + 1],
            )
        nc.vector.tensor_reduce(out=neg[:, 2:3], in_=scores[1], axis=ALONG_FREE, op=ALU.max, negate=True)
        nc.scalar.activation(
            out=p[1][:].rearrange("q (u s e) -> q u s e", u=2, e=2), in_=dealt(1),
            func=ACT.Exp, bias=neg[:, 2:3], scale=1.0, accum_out=sums[:, 2:3],
        )
        nc.vector.tensor_reduce(out=neg[:, 3:4], in_=scores[last], axis=ALONG_FREE, op=ALU.max, negate=True)
        exp_half(last, 0, p_last[0][:], 3)

        w0 = sb.tile([P, PAGE], F32, name="w0", align_bytes=64)
        w10 = sb.tile([P, HALF], F32, name="w10", align_bytes=64)
        weigh(0, 0, w0[:, :HALF])
        nc.vector.tensor_reduce(out=neg_max, in_=neg[:, :parts], axis=ALONG_FREE, op=ALU.min)
        nc.scalar.activation(out=lift[:], in_=neg[:], func=ACT.Exp, bias=neg_max, scale=-1.0)
        exp_half(last, 1, p_last[1][:], parts)
        weigh(0, 1, w0[:, HALF:])
        weigh(1, 0, w10[:])

        nc.vector.tensor_scalar(out=pairs[1][0], in0=w10[:], scalar1=lift[:, 2:3], scalar2=None, op0=ALU.mult)
        weigh_and_round(1, 1, p[1][:, HALF:], 2)
        for h in range(2):
            nc.scalar.activation(out=words_of_half(pairs_first, h), in_=words_of_half(w0, h), func=ACT.Copy, scale=lift[:, h : h + 1])
        weigh_and_round(last, 0, p_last[0][:], 3)
        weigh_and_round(last, 1, p_last[1][:], parts)

        def query_cuts(g):
            return ((0, NQ // 2), (NQ // 2, NQ)) if g == last else ((0, NQ),)

        order = (1, 0, last)
        w_bf = {}
        for g in order:
            turned = ps.tile([P, 2, NQ], F32, name=f"turned{g}", tag=f"turn{g}")
            for u in range(2):
                nc.tensor.transpose(turned[:, u, :], pairs[g][u].bitcast(F32), ident[:])
            w_bf[g] = sb.tile([P, NQ * PACK], BF16, name=f"w_bf{g}", tag=f"w_bf{g}", align_bytes=64)
            for a, b in query_cuts(g):
                nc.scalar.copy(out=w_bf[g][:, PACK * a : PACK * b].bitcast(F32).rearrange("s (q u) -> s q u", u=2), in_=turned[:, :, a:b].rearrange("s u q -> s q u"))

        v_all = laid.tile([P, PAGES * DV], U32, name="v_all", align_bytes=64, offset=P_LAST_AT)
        nc.vector.tensor_copy(v_all[:], v_pool[:].bitcast(U32).indirect(v_list[:]))
        v_codes = [v_all[:, g * DV : (g + 1) * DV] for g in range(PAGES)]

        cols_half = DV // 2
        acc = [ps.tile([P, cols_half], F32, name=f"acc{h}", tag=("acc", "turn3")[h]) for h in range(2)]
        for g in order:
            w_codes = sb.tile([P, NQ], U32, name=f"w_codes{g}", align_bytes=64)
            w_plane = sb.tile([P, NQ], U8, name=f"w_plane{g}", align_bytes=64)
            for a, b in query_cuts(g):
                nc.vector.quantize_mx(out=w_codes[:, a:b].bitcast(FP8X4), scales=w_plane[:, a:b], in_=w_bf[g][:, PACK * a : PACK * b])
            for h in range(2):
                cols = slice(g * DV + h * cols_half, g * DV + (h + 1) * cols_half)
                nc.tensor.matmul_mx(
                    out=acc[h][:], lhsT=w_codes[:].bitcast(FP8X4), lhsT_scale=w_plane[:],
                    rhs=v_codes[g][:, h * cols_half : (h + 1) * cols_half].bitcast(FP8X4), rhs_scale=v_plane[:, cols],
                    start=(g == order[0]), stop=(g == last),
                )

        total = sb.tile([P, 1], F32, name="total")
        lifted = sb.tile([P, parts + 1], F32, name="lifted", tag=f"pairs{last}_1", align_bytes=64)
        nc.vector.scalar_tensor_tensor(out=lifted[:], in0=sums[:], scalar=1.0, in1=lift[:], op0=ALU.mult, op1=ALU.mult, accum_out=total[:])
        inv = sb.tile([P, 1], F32, name="inv", tag=f"w_bf{last}", align_bytes=64)
        nc.vector.reciprocal(inv[:], total[:])

        y0 = sb.tile([P, cols_half], F32, name="y0")
        y1 = sb.tile([P, cols_half], F32, name="y1")
        nc.scalar.activation(out=y0[:], in_=acc[0][:], func=ACT.Copy, scale=inv[:])
        nc.vector.tensor_scalar(out=y1[:], in0=acc[1][:], scalar1=inv[:], scalar2=None, op0=ALU.mult)
        nc.scalar.dma_start(out=out[0, :, :cols_half], in_=y0[:])
        nc.sync.dma_start(out=out[0, :, cols_half:], in_=y1[:])
